import numpy as np
import ml_dtypes


def mxq(x, axis, fmt="e4m3"):
    dtype, down = {"e4m3": (ml_dtypes.float8_e4m3fn, 7), "e5m2": (ml_dtypes.float8_e5m2, 14)}[fmt]
    v = np.moveaxis(np.asarray(x, np.float32).astype(ml_dtypes.bfloat16).astype(np.float64), axis, -1)
    blocks = v.reshape(v.shape[:-1] + (-1, 32))
    amax = np.abs(blocks).max(-1, keepdims=True)
    byte = np.maximum(np.where(amax > 0, np.frexp(amax)[1] - 1 + 127, 0) - down, 1)
    scale = np.exp2(byte - 127.0)
    codes = (blocks / scale).astype(np.float32).astype(dtype).astype(np.float64)
    return np.moveaxis((codes * scale).reshape(v.shape), -1, axis)


WIDE = False


def mx_kscale(k):
    if not WIDE:
        return np.ones(k)
    levels = np.array([24, -24, 12, -12, 0])
    if k % 512:
        return np.exp2(np.random.permutation(np.resize(levels, k // 32))).repeat(32)
    a = np.empty((k // 512, 16))
    for p in range(k // 512):
        a[p, :8] = np.random.permutation(np.resize(levels, 8))
        for g in range(8):
            far = levels[np.abs(levels - a[p, g]) >= 10]
            a[p, g + 8] = far[np.random.randint(len(far))]
    return np.exp2(a.ravel()).repeat(32)


def f64(x):
    return np.asarray(x).astype(np.float64)


def striped(idx):
    return np.tile(idx.reshape(-1, 16).T, (8, 1)).astype(np.uint16)


def unstriped(offs):
    return offs[:16].T.reshape(-1).astype(np.int64)


E2M1 = np.array([0.0, 0.5, 1.0, 1.5, 2.0, 3.0, 4.0, 6.0, -0.0, -0.5, -1.0, -1.5, -2.0, -3.0, -4.0, -6.0])


def pack_weight(w, fmt):
    k, n = w.shape
    w = f64(np.asarray(w, np.float32).astype(ml_dtypes.bfloat16)).reshape(k // 32, 32, n)
    amax = np.abs(w).max(1)
    if fmt == "e4m3":
        byte = np.frexp(amax)[1] - 1 + 127 - 7
    else:
        mant, ex = np.frexp(amax / 6.0)
        byte = np.where(mant > 0.5, ex, ex - 1) + 127
    byte = np.clip(np.where(amax > 0, byte, 1), 1, 254)
    scaled = (w * np.exp2(127.0 - byte)[:, None, :]).reshape(k, n).astype(np.float32)
    by_word = np.ascontiguousarray(scaled.reshape(k // 512, 128, 4, n).transpose(0, 1, 3, 2))
    if fmt == "e4m3":
        words = by_word.astype(ml_dtypes.float8_e4m3fn).view(np.uint8)
    else:
        c = by_word.astype(ml_dtypes.float4_e2m1fn).view(np.uint8) & 0xF
        words = (c[..., 0::2] | (c[..., 1::2] << 4)).reshape(k // 512, 128, 2 * n)
    return np.ascontiguousarray(words), np.ascontiguousarray(byte.astype(np.uint8).reshape(k // 512, 16, n))


def unpack_weight(words, scales, fmt):
    g, _, n = scales.shape
    words = np.ascontiguousarray(words).reshape(g, 128, n, -1)
    if fmt == "e4m3":
        vals = words.view(ml_dtypes.float8_e4m3fn).astype(np.float64)
    else:
        nib = np.empty((g, 128, n, 4), np.uint8)
        nib[..., 0::2] = words & 0xF
        nib[..., 1::2] = words >> 4
        vals = E2M1[nib]
    vals = vals * np.repeat(np.exp2(scales.astype(np.float64) - 127.0), 8, axis=1)[..., None]
    return vals.transpose(0, 1, 3, 2).reshape(g * 512, n)


K, L, N, T, J = 512, 512, 512, 2048, 512


def setup_inputs():
    n = np.random.standard_normal
    s = mx_kscale(K)[:, None]
    s2 = mx_kscale(L)[:, None]
    p_tab = pack_weight(n((K, T)) * s, "e4m3")
    p_w = pack_weight(n((K, N)) / np.sqrt(K) / s, "e4m3")
    p_wx = pack_weight(n((L, N)) / np.sqrt(L) / s2, "e2m1")
    return {
        "tab_words": p_tab[0],
        "tab_scales": p_tab[1],
        "w_words": p_w[0],
        "w_scales": p_w[1],
        "x": (n((L, J)) * s2).astype(np.float32),
        "wx_words": p_wx[0],
        "wx_scales": p_wx[1],
        "iw0": (np.random.uniform(0.1, 0.6, J)).astype(np.float32),
        "iw1": (np.random.uniform(0.1, 0.6, J)).astype(np.float32),
        "res": (n((N, J))).astype(np.float32),
        "offs": striped(np.concatenate([np.random.permutation(T)[:J] for _ in range(2)])),
    }


def reference(tab_words, tab_scales, w_words, w_scales, x, wx_words, wx_scales, iw0, iw1, res, offs):
    idx = unstriped(offs).reshape(2, J)
    tab_ = unpack_weight(tab_words, tab_scales, "e4m3")[:, idx]
    w_ = unpack_weight(w_words, w_scales, "e4m3")
    a0 = w_.T @ tab_[:, 0]
    a1 = w_.T @ tab_[:, 1]
    x_ = mxq(f64(x), 0, "e4m3")
    wx_ = unpack_weight(wx_words, wx_scales, "e2m1")
    ax = wx_.T @ x_
    return a0 * f64(iw0)[None, :] + a1 * f64(iw1)[None, :] + ax + f64(res)

@@ -1,0 +1,195 @@
+from contextlib import ExitStack
+
+import concourse.mybir as mybir
+from concourse.masks import make_identity
+
+K, L, N, T, J = 512, 512, 512, 2048, 512
+FLOPS = 2 * 3 * K * N * J
+
+F32 = mybir.dt.float32
+BF16 = mybir.dt.bfloat16
+I32 = mybir.dt.int32
+U32 = mybir.dt.uint32
+U16 = mybir.dt.uint16
+U8 = mybir.dt.uint8
+FP8X4 = mybir.dt.float8_e4m3fn_x4
+FP4X4 = mybir.dt.float4_e2m1fn_x4
+COPY = mybir.ActivationFunctionType.Copy
+MULT = mybir.AluOpType.mult
+ADD = mybir.AluOpType.add
+
+P = 128
+PACK = 4
+HALF = J // 2
+CHUNKS = J // P
+NT = N // P
+
+
+def tile_list_interp_res_kernel(tc, tab_words, tab_scales, w_words, w_scales, x, wx_words, wx_scales, iw0, iw1, res, offs, out):
+    nc = tc.nc
+    with ExitStack() as ctx:
+        keep = ctx.enter_context(tc.tile_pool(name="keep", bufs=1))
+        acc_pool = ctx.enter_context(tc.psum_pool(name="acc", bufs=4))
+        sum_pool = ctx.enter_context(tc.psum_pool(name="sums", bufs=1))
+
+        offsets = keep.tile([P, 2 * J // 16], U16, name="offsets")
+        tab_plane = keep.tile([P, T // 4], I32, name="tab_plane", align_bytes=64)
+        w_plane = keep.tile([P, N // 4], I32, name="w_plane", align_bytes=64)
+        wx_plane = keep.tile([P, N // 4], I32, name="wx_plane", align_bytes=64)
+        tab_codes = keep.tile([P, T], I32, name="tab_codes", align_bytes=64)
+        w_codes = keep.tile([P, N], I32, name="w_codes", align_bytes=64)
+        wx_codes = keep.tile([P, N // 2], I32, name="wx_codes", align_bytes=64)
+        ident = keep.tile([P, P], F32, name="ident")
+        iw_rows = keep.tile([P, P], F32, name="iw_rows")
+        iw_cols = keep.tile([P, 2 * CHUNKS], F32, name="iw_cols")
+        x_raw = [keep.tile([P, PACK, HALF], F32, name=f"x_raw{h}") for h in range(2)]
+        x_bf = [keep.tile([P, HALF, PACK], BF16, name=f"x_bf{h}", align_bytes=64) for h in range(2)]
+        x_codes = [keep.tile([P, HALF], U32, name=f"x_codes{h}", align_bytes=64) for h in range(2)]
+        x_plane = [keep.tile([P, HALF], U8, name=f"x_plane{h}", align_bytes=64) for h in range(2)]
+        res_sb = [keep.tile([P, NT, HALF], F32, name=f"res{h}") for h in range(2)]
+        got_codes = [[keep.tile([P, HALF], U32, name=f"got_codes{g}{h}", align_bytes=64) for h in range(2)] for g in range(2)]
+        got_plane = [[keep.tile([P, HALF], U8, name=f"got_plane{g}{h}", align_bytes=64) for h in range(2)] for g in range(2)]
+        sums = [sum_pool.tile([P, NT, P], F32, name=f"sums{c}") for c in range(CHUNKS)]
+
+        def load_plane(queue, plane, scales):
+            rows = scales[0].bitcast(I32)
+            for q in range(4):
+                queue.dma_start(out=plane[32 * q : 32 * q + 4, :], in_=rows[4 * q : 4 * q + 4, :])
+
+        x_view = x.rearrange("(p t) j -> p t j", t=PACK)
+        res_view = res.rearrange("(a p) j -> p a j", p=P)
+        out_view = out.rearrange("(a p) j -> p a j", p=P)
+
+        nc.vector.memset(tab_plane[:], 0)
+        nc.vector.memset(w_plane[:], 0)
+        nc.gpsimd.memset(wx_plane[:], 0)
+        make_identity(nc, ident[:])
+
+        nc.sync.dma_start(offsets[:], offs)
+        load_plane(nc.scalar, tab_plane, tab_scales)
+        nc.sync.dma_start(out=x_raw[0][:], in_=x_view[:, :, 0:HALF])
+        nc.sync.dma_start(out=wx_codes[:], in_=wx_words[0].bitcast(I32))
+        nc.sync.dma_start(out=tab_codes[:], in_=tab_words[0].rearrange("p t i -> p (t i)").bitcast(I32))
+        load_plane(nc.sync, w_plane, w_scales)
+        nc.sync.dma_start(out=w_codes[:], in_=w_words[0].rearrange("p n i -> p (n i)").bitcast(I32))
+        nc.sync.dma_start(out=x_raw[1][:], in_=x_view[:, :, HALF:J])
+        for h in range(2):
+            nc.sync.dma_start(out=res_sb[h][:], in_=res_view[:, :, h * HALF : (h + 1) * HALF])
+        load_plane(nc.gpsimd, wx_plane, wx_scales)
+        nc.scalar.activation(out=iw_rows[:], in_=ident[:], func=COPY)
+        for g, iw in enumerate((iw0, iw1)):
+            nc.gpsimd.dma_start(out=iw_rows[CHUNKS * g : CHUNKS * (g + 1), :], in_=iw.rearrange("(c p) -> c p", p=P))
+
+        def list_slice(g, h):
+            first = (g * J + h * HALF) // 16
+            return offsets[:, first : first + HALF // 16]
+
+        def gather_plane(g, h):
+            nc.vector.tensor_copy(got_plane[g][h][:], tab_plane[:].bitcast(U8).indirect(list_slice(g, h)))
+
+        def gather_codes(g, h):
+            nc.vector.tensor_copy(got_codes[g][h][:], tab_codes[:].bitcast(U32).indirect(list_slice(g, h)))
+
+        def interleave(copy, h):
+            copy(
+                out=x_bf[h][:].rearrange("p (c i) t -> p c t i", i=4),
+                in_=x_raw[h][:].rearrange("p t (c i) -> p c t i", i=4),
+            )
+
+        def quantize(h):
+            nc.vector.quantize_mx(
+                out=x_codes[h][:].bitcast(FP8X4),
+                scales=x_plane[h][:],
+                in_=x_bf[h][:].rearrange("p j t -> p (j t)"),
+            )
+
+        def product(codes, plane, c, weights, weights_plane):
+            cols = slice((c % 2) * P, (c % 2 + 1) * P)
+            acc = acc_pool.tile([P, N], F32, name="acc")
+            nc.tensor.matmul_mx(
+                out=acc[:],
+                lhsT=codes[c // 2][:, cols].bitcast(FP8X4),
+                lhsT_scale=plane[c // 2][:, cols],
+                rhs=weights,
+                rhs_scale=weights_plane[:].bitcast(U8),
+                start=True,
+                stop=True,
+            )
+            return acc
+
+        def table_product(g, c):
+            return product(got_codes[g], got_plane[g], c, w_codes[:].bitcast(FP8X4), w_plane)
+
+        def skip_product(c):
+            return product(x_codes, x_plane, c, wx_codes[:].bitcast(FP4X4), wx_plane)
+
+        def term_tile(kind, c):
+            return keep.tile([P, N], F32, name=f"term_{kind}{c}")
+
+        def turn(term, c, first, last):
+            for a in range(NT):
+                nc.tensor.matmul(
+                    out=sums[c][:, a, :],
+                    lhsT=term[:, a * P : (a + 1) * P],
+                    rhs=ident[:],
+                    is_transpose=True,
+                    start=first and a == 0,
+                    stop=last and a == NT - 1,
+                )
+
+        def weight(g, c):
+            return iw_cols[:, CHUNKS * g + c : CHUNKS * g + c + 1]
+
+        def finish(c):
+            done = keep.tile([P, NT, P], F32, name=f"done{c}")
+            cols = slice((c % 2) * P, (c % 2 + 1) * P)
+            nc.vector.tensor_tensor(done[:], sums[c][:], res_sb[c // 2][:, :, cols], ADD)
+            nc.sync.dma_start(out=out_view[:, :, c * P : (c + 1) * P], in_=done[:])
+
+        gather_plane(0, 0)
+        gather_plane(1, 0)
+        interleave(nc.scalar.copy, 0)
+        gather_plane(0, 1)
+        quantize(0)
+        gather_plane(1, 1)
+        skip = {}
+        for c in (0, 1):
+            acc = skip_product(c)
+            skip[c] = term_tile("x", c)
+            nc.scalar.copy(out=skip[c][:], in_=acc[:])
+        iw_acc = acc_pool.tile([P, N], F32, name="acc")
+        nc.tensor.transpose(iw_acc[:, 0:P], iw_rows[:], ident[:])
+        nc.scalar.copy(out=iw_cols[:], in_=iw_acc[:, 0 : 2 * CHUNKS])
+        for h in range(2):
+            for g in range(2):
+                gather_codes(g, h)
+        terms = {}
+        for g in range(2):
+            for c in (0, 1):
+                acc = table_product(g, c)
+                terms[g, c] = term_tile(f"g{g}", c)
+                nc.scalar.activation(out=terms[g, c][:], in_=acc[:], func=COPY, scale=weight(g, c))
+        interleave(nc.vector.tensor_copy, 1)
+        for c in (2, 3):
+            acc = table_product(0, c)
+            terms[0, c] = term_tile("g0", c)
+            nc.scalar.activation(out=terms[0, c][:], in_=acc[:], func=COPY, scale=weight(0, c))
+        for c in (0, 1):
+            turn(skip[c], c, True, False)
+            turn(terms[0, c], c, False, False)
+            turn(terms[1, c], c, False, True)
+        quantize(1)
+        late = {c: table_product(1, c) for c in (2, 3)}
+        finish(0)
+        for c in (2, 3):
+            acc = skip_product(c)
+            skip[c] = term_tile("x", c)
+            nc.scalar.copy(out=skip[c][:], in_=acc[:])
+        for c in (2, 3):
+            terms[1, c] = term_tile("g1", c)
+            nc.vector.scalar_tensor_tensor(terms[1, c][:], late[c][:], weight(1, c), terms[0, c][:], MULT, ADD)
+        finish(1)
+        for c in (2, 3):
+            turn(terms[1, c], c, True, False)
+            turn(skip[c], c, False, True)
+            finish(c)

@@ -43,7 +43,7 @@ def tile_list_interp_res_kernel(tc, tab_words, tab_scales, w_words, w_scales, x,
         iw_rows = keep.tile([P, P], F32, name="iw_rows")
         iw_cols = keep.tile([P, 2 * CHUNKS], F32, name="iw_cols")
         x_raw = [keep.tile([P, PACK, HALF], F32, name=f"x_raw{h}") for h in range(2)]
-        x_bf = [keep.tile([P, HALF, PACK], BF16, name=f"x_bf{h}", align_bytes=64) for h in range(2)]
+        x_bf = [keep.tile([P, P, PACK], BF16, name=f"x_bf{c}", align_bytes=64) for c in range(CHUNKS)]
         x_codes = [keep.tile([P, HALF], U32, name=f"x_codes{h}", align_bytes=64) for h in range(2)]
         x_plane = [keep.tile([P, HALF], U8, name=f"x_plane{h}", align_bytes=64) for h in range(2)]
         res_sb = [keep.tile([P, NT, HALF], F32, name=f"res{h}") for h in range(2)]
@@ -61,24 +61,25 @@ def tile_list_interp_res_kernel(tc, tab_words, tab_scales, w_words, w_scales, x,
         out_view = out.rearrange("(a p) j -> p a j", p=P)
 
         nc.vector.memset(tab_plane[:], 0)
+        nc.vector.memset(wx_plane[:], 0)
         nc.vector.memset(w_plane[:], 0)
-        nc.gpsimd.memset(wx_plane[:], 0)
         make_identity(nc, ident[:])
 
-        nc.sync.dma_start(offsets[:], offs)
-        load_plane(nc.scalar, tab_plane, tab_scales)
-        nc.sync.dma_start(out=x_raw[0][:], in_=x_view[:, :, 0:HALF])
+        nc.scalar.activation(out=iw_rows[:], in_=ident[:], func=COPY)
+
         nc.sync.dma_start(out=wx_codes[:], in_=wx_words[0].bitcast(I32))
+        nc.sync.dma_start(offsets[:], offs)
+        load_plane(nc.sync, tab_plane, tab_scales)
+        for h in range(2):
+            nc.sync.dma_start(out=x_raw[h][:], in_=x_view[:, :, h * HALF : (h + 1) * HALF])
+        load_plane(nc.sync, wx_plane, wx_scales)
         nc.sync.dma_start(out=tab_codes[:], in_=tab_words[0].rearrange("p t i -> p (t i)").bitcast(I32))
+        for g, iw in enumerate((iw0, iw1)):
+            nc.sync.dma_start(out=iw_rows[CHUNKS * g : CHUNKS * (g + 1), :], in_=iw.rearrange("(c p) -> c p", p=P))
         load_plane(nc.sync, w_plane, w_scales)
         nc.sync.dma_start(out=w_codes[:], in_=w_words[0].rearrange("p n i -> p (n i)").bitcast(I32))
-        nc.sync.dma_start(out=x_raw[1][:], in_=x_view[:, :, HALF:J])
         for h in range(2):
             nc.sync.dma_start(out=res_sb[h][:], in_=res_view[:, :, h * HALF : (h + 1) * HALF])
-        load_plane(nc.gpsimd, wx_plane, wx_scales)
-        nc.scalar.activation(out=iw_rows[:], in_=ident[:], func=COPY)
-        for g, iw in enumerate((iw0, iw1)):
-            nc.gpsimd.dma_start(out=iw_rows[CHUNKS * g : CHUNKS * (g + 1), :], in_=iw.rearrange("(c p) -> c p", p=P))
 
         def list_slice(g, h):
             first = (g * J + h * HALF) // 16
@@ -90,17 +91,19 @@ def tile_list_interp_res_kernel(tc, tab_words, tab_scales, w_words, w_scales, x,
         def gather_codes(g, h):
             nc.vector.tensor_copy(got_codes[g][h][:], tab_codes[:].bitcast(U32).indirect(list_slice(g, h)))
 
-        def interleave(copy, h):
+        def interleave(copy, c):
+            cols = slice((c % 2) * P, (c % 2 + 1) * P)
             copy(
-                out=x_bf[h][:].rearrange("p (c i) t -> p c t i", i=4),
-                in_=x_raw[h][:].rearrange("p t (c i) -> p c t i", i=4),
+                out=x_bf[c][:].rearrange("p (c i) t -> p c t i", i=4),
+                in_=x_raw[c // 2][:, :, cols].rearrange("p t (c i) -> p c t i", i=4),
             )
 
-        def quantize(h):
+        def quantize(c):
+            cols = slice((c % 2) * P, (c % 2 + 1) * P)
             nc.vector.quantize_mx(
-                out=x_codes[h][:].bitcast(FP8X4),
-                scales=x_plane[h][:],
-                in_=x_bf[h][:].rearrange("p j t -> p (j t)"),
+                out=x_codes[c // 2][:, cols].bitcast(FP8X4),
+                scales=x_plane[c // 2][:, cols],
+                in_=x_bf[c][:].rearrange("p j t -> p (j t)"),
             )
 
         def product(codes, plane, c, weights, weights_plane):
@@ -146,50 +149,50 @@ def tile_list_interp_res_kernel(tc, tab_words, tab_scales, w_words, w_scales, x,
             nc.vector.tensor_tensor(done[:], sums[c][:], res_sb[c // 2][:, :, cols], ADD)
             nc.sync.dma_start(out=out_view[:, :, c * P : (c + 1) * P], in_=done[:])
 
-        gather_plane(0, 0)
-        gather_plane(1, 0)
-        interleave(nc.scalar.copy, 0)
-        gather_plane(0, 1)
+        for h in range(2):
+            for g in range(2):
+                gather_plane(g, h)
+        for c in range(3):
+            interleave(nc.scalar.copy, c)
         quantize(0)
-        gather_plane(1, 1)
+        interleave(nc.vector.tensor_copy, 3)
+        for c in (1, 2, 3):
+            quantize(c)
         skip = {}
-        for c in (0, 1):
+        for c in range(CHUNKS):
             acc = skip_product(c)
             skip[c] = term_tile("x", c)
-            nc.scalar.copy(out=skip[c][:], in_=acc[:])
+            copy = nc.vector.tensor_copy if c == 1 else nc.scalar.copy
+            copy(out=skip[c][:], in_=acc[:])
         iw_acc = acc_pool.tile([P, N], F32, name="acc")
         nc.tensor.transpose(iw_acc[:, 0:P], iw_rows[:], ident[:])
         nc.scalar.copy(out=iw_cols[:], in_=iw_acc[:, 0 : 2 * CHUNKS])
+        for c in range(CHUNKS):
+            turn(skip[c], c, True, False)
         for h in range(2):
             for g in range(2):
                 gather_codes(g, h)
         terms = {}
-        for g in range(2):
-            for c in (0, 1):
-                acc = table_product(g, c)
-                terms[g, c] = term_tile(f"g{g}", c)
-                nc.scalar.activation(out=terms[g, c][:], in_=acc[:], func=COPY, scale=weight(g, c))
-        interleave(nc.vector.tensor_copy, 1)
-        for c in (2, 3):
-            acc = table_product(0, c)
-            terms[0, c] = term_tile("g0", c)
-            nc.scalar.activation(out=terms[0, c][:], in_=acc[:], func=COPY, scale=weight(0, c))
+
+        def scaled(g, c):
+            acc = table_product(g, c)
+            terms[g, c] = term_tile(f"g{g}", c)
+            nc.scalar.activation(out=terms[g, c][:], in_=acc[:], func=COPY, scale=weight(g, c))
+
         for c in (0, 1):
-            turn(skip[c], c, True, False)
-            turn(terms[0, c], c, False, False)
-            turn(terms[1, c], c, False, True)
-        quantize(1)
-        late = {c: table_product(1, c) for c in (2, 3)}
-        finish(0)
-        for c in (2, 3):
-            acc = skip_product(c)
-            skip[c] = term_tile("x", c)
-            nc.scalar.copy(out=skip[c][:], in_=acc[:])
-        for c in (2, 3):
+            scaled(0, c)
+        for c in (0, 1):
+            acc = table_product(1, c)
             terms[1, c] = term_tile("g1", c)
-            nc.vector.scalar_tensor_tensor(terms[1, c][:], late[c][:], weight(1, c), terms[0, c][:], MULT, ADD)
-        finish(1)
+            nc.vector.scalar_tensor_tensor(terms[1, c][:], acc[:], weight(1, c), terms[0, c][:], MULT, ADD)
+        for g in range(2):
+            for c in (2, 3):
+                scaled(g, c)
+        for c in (0, 1):
+            turn(terms[1, c], c, False, True)
+            finish(c)
         for c in (2, 3):
-            turn(terms[1, c], c, True, False)
-            turn(skip[c], c, False, True)
+            turn(terms[0, c], c, False, False)
+        for c in (2, 3):
+            turn(terms[1, c], c, False, True)
             finish(c)

@@ -46,7 +46,7 @@ def tile_list_interp_res_kernel(tc, tab_words, tab_scales, w_words, w_scales, x,
         x_bf = [keep.tile([P, P, PACK], BF16, name=f"x_bf{c}", align_bytes=64) for c in range(CHUNKS)]
         x_codes = [keep.tile([P, HALF], U32, name=f"x_codes{h}", align_bytes=64) for h in range(2)]
         x_plane = [keep.tile([P, HALF], U8, name=f"x_plane{h}", align_bytes=64) for h in range(2)]
-        res_sb = [keep.tile([P, NT, HALF], F32, name=f"res{h}") for h in range(2)]
+        res_sb = keep.tile([P, NT, J], F32, name="res_sb")
         got_codes = [[keep.tile([P, HALF], U32, name=f"got_codes{g}{h}", align_bytes=64) for h in range(2)] for g in range(2)]
         got_plane = [[keep.tile([P, HALF], U8, name=f"got_plane{g}{h}", align_bytes=64) for h in range(2)] for g in range(2)]
         sums = [sum_pool.tile([P, NT, P], F32, name=f"sums{c}") for c in range(CHUNKS)]
@@ -63,10 +63,10 @@ def tile_list_interp_res_kernel(tc, tab_words, tab_scales, w_words, w_scales, x,
         nc.vector.memset(tab_plane[:], 0)
         nc.vector.memset(wx_plane[:], 0)
         nc.vector.memset(w_plane[:], 0)
+        nc.gpsimd.memset(iw_rows[:], 0.0)
         make_identity(nc, ident[:])
 
-        nc.scalar.activation(out=iw_rows[:], in_=ident[:], func=COPY)
-
+        nc.sync.dma_start(out=w_codes[:], in_=w_words[0].rearrange("p n i -> p (n i)").bitcast(I32))
         nc.sync.dma_start(out=wx_codes[:], in_=wx_words[0].bitcast(I32))
         nc.sync.dma_start(offsets[:], offs)
         load_plane(nc.sync, tab_plane, tab_scales)
@@ -77,9 +77,10 @@ def tile_list_interp_res_kernel(tc, tab_words, tab_scales, w_words, w_scales, x,
         for g, iw in enumerate((iw0, iw1)):
             nc.sync.dma_start(out=iw_rows[CHUNKS * g : CHUNKS * (g + 1), :], in_=iw.rearrange("(c p) -> c p", p=P))
         load_plane(nc.sync, w_plane, w_scales)
-        nc.sync.dma_start(out=w_codes[:], in_=w_words[0].rearrange("p n i -> p (n i)").bitcast(I32))
-        for h in range(2):
-            nc.sync.dma_start(out=res_sb[h][:], in_=res_view[:, :, h * HALF : (h + 1) * HALF])
+        nc.sync.dma_start(out=res_sb[:], in_=res_view)
+
+        def scalar_copy(out, in_):
+            nc.scalar.activation(out=out, in_=in_, func=COPY)
 
         def list_slice(g, h):
             first = (g * J + h * HALF) // 16
@@ -143,32 +144,29 @@ def tile_list_interp_res_kernel(tc, tab_words, tab_scales, w_words, w_scales, x,
         def weight(g, c):
             return iw_cols[:, CHUNKS * g + c : CHUNKS * g + c + 1]
 
-        def finish(c):
-            done = keep.tile([P, NT, P], F32, name=f"done{c}")
-            cols = slice((c % 2) * P, (c % 2 + 1) * P)
-            nc.vector.tensor_tensor(done[:], sums[c][:], res_sb[c // 2][:, :, cols], ADD)
-            nc.sync.dma_start(out=out_view[:, :, c * P : (c + 1) * P], in_=done[:])
+        def finish(c, tiles):
+            done = keep.tile([P, len(tiles), P], F32, name=f"done{c}_{tiles.start}")
+            rows = slice(tiles.start, tiles.stop)
+            cols = slice(c * P, (c + 1) * P)
+            nc.vector.tensor_tensor(done[:], sums[c][:, rows, :], res_sb[:, rows, cols], ADD)
+            nc.sync.dma_start(out=out_view[:, rows, cols], in_=done[:])
 
         for h in range(2):
             for g in range(2):
                 gather_plane(g, h)
-        for c in range(3):
-            interleave(nc.scalar.copy, c)
-        quantize(0)
-        interleave(nc.vector.tensor_copy, 3)
-        for c in (1, 2, 3):
+        for c in range(CHUNKS):
+            interleave(scalar_copy, c)
             quantize(c)
         skip = {}
         for c in range(CHUNKS):
             acc = skip_product(c)
             skip[c] = term_tile("x", c)
-            copy = nc.vector.tensor_copy if c == 1 else nc.scalar.copy
-            copy(out=skip[c][:], in_=acc[:])
+            scalar_copy(out=skip[c][:], in_=acc[:])
+        for c in (0, 1):
+            turn(skip[c], c, True, False)
         iw_acc = acc_pool.tile([P, N], F32, name="acc")
         nc.tensor.transpose(iw_acc[:, 0:P], iw_rows[:], ident[:])
-        nc.scalar.copy(out=iw_cols[:], in_=iw_acc[:, 0 : 2 * CHUNKS])
-        for c in range(CHUNKS):
-            turn(skip[c], c, True, False)
+        scalar_copy(out=iw_cols[:], in_=iw_acc[:, 0 : 2 * CHUNKS])
         for h in range(2):
             for g in range(2):
                 gather_codes(g, h)
@@ -179,20 +177,25 @@ def tile_list_interp_res_kernel(tc, tab_words, tab_scales, w_words, w_scales, x,
             terms[g, c] = term_tile(f"g{g}", c)
             nc.scalar.activation(out=terms[g, c][:], in_=acc[:], func=COPY, scale=weight(g, c))
 
+        def fused(g, c, other):
+            acc = table_product(g, c)
+            terms[g, c] = term_tile(f"g{g}", c)
+            nc.vector.scalar_tensor_tensor(terms[g, c][:], acc[:], weight(g, c), other[:], MULT, ADD)
+
         for c in (0, 1):
             scaled(0, c)
         for c in (0, 1):
-            acc = table_product(1, c)
-            terms[1, c] = term_tile("g1", c)
-            nc.vector.scalar_tensor_tensor(terms[1, c][:], acc[:], weight(1, c), terms[0, c][:], MULT, ADD)
-        for g in range(2):
-            for c in (2, 3):
-                scaled(g, c)
+            fused(1, c, terms[0, c])
+        for c in (2, 3):
+            fused(0, c, skip[c])
+        for c in (2, 3):
+            scaled(1, c)
         for c in (0, 1):
             turn(terms[1, c], c, False, True)
-            finish(c)
         for c in (2, 3):
-            turn(terms[0, c], c, False, False)
-        for c in (2, 3):
-            turn(terms[1, c], c, False, True)
-            finish(c)
+            turn(terms[1, c], c, True, False)
+            turn(terms[0, c], c, False, True)
+        for c in range(CHUNKS - 1):
+            finish(c, range(NT))
+        finish(CHUNKS - 1, range(0, NT // 2))
+        finish(CHUNKS - 1, range(NT // 2, NT))

@@ -53,8 +53,8 @@ def tile_list_interp_res_kernel(tc, tab_words, tab_scales, w_words, w_scales, x,
 
         def load_plane(queue, plane, scales):
             rows = scales[0].bitcast(I32)
-            for q in range(4):
-                queue.dma_start(out=plane[32 * q : 32 * q + 4, :], in_=rows[4 * q : 4 * q + 4, :])
+            for r in range(4):
+                queue.dma_start(out=plane[r:P:32, :], in_=rows[r:16:4, :])
 
         x_view = x.rearrange("(p t) j -> p t j", t=PACK)
         res_view = res.rearrange("(a p) j -> p a j", p=P)

@@ -48,7 +48,7 @@ def tile_list_interp_res_kernel(tc, tab_words, tab_scales, w_words, w_scales, x,
         x_plane = [keep.tile([P, HALF], U8, name=f"x_plane{h}", align_bytes=64) for h in range(2)]
         res_sb = keep.tile([P, NT, J], F32, name="res_sb")
         got_codes = [[keep.tile([P, HALF], U32, name=f"got_codes{g}{h}", align_bytes=64) for h in range(2)] for g in range(2)]
-        got_plane = [[keep.tile([P, HALF], U8, name=f"got_plane{g}{h}", align_bytes=64) for h in range(2)] for g in range(2)]
+        got_plane = [[None, None], [None, None]]
         sums = [sum_pool.tile([P, NT, P], F32, name=f"sums{c}") for c in range(CHUNKS)]
 
         def load_plane(queue, plane, scales):
@@ -66,14 +66,14 @@ def tile_list_interp_res_kernel(tc, tab_words, tab_scales, w_words, w_scales, x,
         nc.gpsimd.memset(iw_rows[:], 0.0)
         make_identity(nc, ident[:])
 
-        nc.sync.dma_start(out=w_codes[:], in_=w_words[0].rearrange("p n i -> p (n i)").bitcast(I32))
-        nc.sync.dma_start(out=wx_codes[:], in_=wx_words[0].bitcast(I32))
         nc.sync.dma_start(offsets[:], offs)
+        nc.sync.dma_start(out=x_raw[0][:], in_=x_view[:, :, 0:HALF])
         load_plane(nc.sync, tab_plane, tab_scales)
-        for h in range(2):
-            nc.sync.dma_start(out=x_raw[h][:], in_=x_view[:, :, h * HALF : (h + 1) * HALF])
+        nc.sync.dma_start(out=wx_codes[:], in_=wx_words[0].bitcast(I32))
+        nc.sync.dma_start(out=x_raw[1][:], in_=x_view[:, :, HALF:J])
         load_plane(nc.sync, wx_plane, wx_scales)
         nc.sync.dma_start(out=tab_codes[:], in_=tab_words[0].rearrange("p t i -> p (t i)").bitcast(I32))
+        nc.sync.dma_start(out=w_codes[:], in_=w_words[0].rearrange("p n i -> p (n i)").bitcast(I32))
         for g, iw in enumerate((iw0, iw1)):
             nc.sync.dma_start(out=iw_rows[CHUNKS * g : CHUNKS * (g + 1), :], in_=iw.rearrange("(c p) -> c p", p=P))
         load_plane(nc.sync, w_plane, w_scales)
@@ -87,6 +87,8 @@ def tile_list_interp_res_kernel(tc, tab_words, tab_scales, w_words, w_scales, x,
             return offsets[:, first : first + HALF // 16]
 
         def gather_plane(g, h):
+            tag = f"got_plane{g}" if h == 0 else f"x_bf{2 + g}"
+            got_plane[g][h] = keep.tile([P, HALF], U8, name=tag, align_bytes=64)
             nc.vector.tensor_copy(got_plane[g][h][:], tab_plane[:].bitcast(U8).indirect(list_slice(g, h)))
 
         def gather_codes(g, h):
@@ -151,17 +153,20 @@ def tile_list_interp_res_kernel(tc, tab_words, tab_scales, w_words, w_scales, x,
             nc.vector.tensor_tensor(done[:], sums[c][:, rows, :], res_sb[:, rows, cols], ADD)
             nc.sync.dma_start(out=out_view[:, rows, cols], in_=done[:])
 
-        for h in range(2):
-            for g in range(2):
-                gather_plane(g, h)
+        for g in range(2):
+            gather_plane(g, 0)
         for c in range(CHUNKS):
             interleave(scalar_copy, c)
             quantize(c)
+        for g in range(2):
+            gather_plane(g, 1)
         skip = {}
-        for c in range(CHUNKS):
-            acc = skip_product(c)
-            skip[c] = term_tile("x", c)
-            scalar_copy(out=skip[c][:], in_=acc[:])
+        for h in range(2):
+            skips = keep.tile([P, 2, N], F32, name=f"x_raw{1 - h}")
+            for c in (2 * h, 2 * h + 1):
+                acc = skip_product(c)
+                skip[c] = skips[:, c % 2, :]
+                scalar_copy(out=skip[c], in_=acc[:])
         for c in (0, 1):
             turn(skip[c], c, True, False)
         iw_acc = acc_pool.tile([P, N], F32, name="acc")
@@ -180,12 +185,12 @@ def tile_list_interp_res_kernel(tc, tab_words, tab_scales, w_words, w_scales, x,
         def fused(g, c, other):
             acc = table_product(g, c)
             terms[g, c] = term_tile(f"g{g}", c)
-            nc.vector.scalar_tensor_tensor(terms[g, c][:], acc[:], weight(g, c), other[:], MULT, ADD)
+            nc.vector.scalar_tensor_tensor(terms[g, c][:], acc[:], weight(g, c), other, MULT, ADD)
 
         for c in (0, 1):
             scaled(0, c)
         for c in (0, 1):
-            fused(1, c, terms[0, c])
+            fused(1, c, terms[0, c][:])
         for c in (2, 3):
             fused(0, c, skip[c])
         for c in (2, 3):

@@ -29,8 +29,7 @@ def tile_list_interp_res_kernel(tc, tab_words, tab_scales, w_words, w_scales, x,
     nc = tc.nc
     with ExitStack() as ctx:
         keep = ctx.enter_context(tc.tile_pool(name="keep", bufs=1))
-        acc_pool = ctx.enter_context(tc.psum_pool(name="acc", bufs=4))
-        sum_pool = ctx.enter_context(tc.psum_pool(name="sums", bufs=1))
+        banks = ctx.enter_context(tc.psum_pool(name="banks", bufs=1))
 
         offsets = keep.tile([P, 2 * J // 16], U16, name="offsets")
         tab_plane = keep.tile([P, T // 4], I32, name="tab_plane", align_bytes=64)
@@ -46,10 +45,10 @@ def tile_list_interp_res_kernel(tc, tab_words, tab_scales, w_words, w_scales, x,
         x_bf = [keep.tile([P, P, PACK], BF16, name=f"x_bf{c}", align_bytes=64) for c in range(CHUNKS)]
         x_codes = [keep.tile([P, HALF], U32, name=f"x_codes{h}", align_bytes=64) for h in range(2)]
         x_plane = [keep.tile([P, HALF], U8, name=f"x_plane{h}", align_bytes=64) for h in range(2)]
-        res_sb = keep.tile([P, NT, J], F32, name="res_sb")
+        res_sb = [keep.tile([P, NT, HALF], F32, name=f"res_sb{h}") for h in range(2)]
         got_codes = [[keep.tile([P, HALF], U32, name=f"got_codes{g}{h}", align_bytes=64) for h in range(2)] for g in range(2)]
         got_plane = [[None, None], [None, None]]
-        sums = [sum_pool.tile([P, NT, P], F32, name=f"sums{c}") for c in range(CHUNKS)]
+        sums = {}
 
         def load_plane(queue, plane, scales):
             rows = scales[0].bitcast(I32)
@@ -77,7 +76,8 @@ def tile_list_interp_res_kernel(tc, tab_words, tab_scales, w_words, w_scales, x,
         for g, iw in enumerate((iw0, iw1)):
             nc.sync.dma_start(out=iw_rows[CHUNKS * g : CHUNKS * (g + 1), :], in_=iw.rearrange("(c p) -> c p", p=P))
         load_plane(nc.sync, w_plane, w_scales)
-        nc.sync.dma_start(out=res_sb[:], in_=res_view)
+        for h in range(2):
+            nc.sync.dma_start(out=res_sb[h][:], in_=res_view[:, :, h * HALF : (h + 1) * HALF])
 
         def scalar_copy(out, in_):
             nc.scalar.activation(out=out, in_=in_, func=COPY)
@@ -109,9 +109,9 @@ def tile_list_interp_res_kernel(tc, tab_words, tab_scales, w_words, w_scales, x,
                 in_=x_bf[c][:].rearrange("p j t -> p (j t)"),
             )
 
-        def product(codes, plane, c, weights, weights_plane):
+        def product(codes, plane, c, weights, weights_plane, bank):
             cols = slice((c % 2) * P, (c % 2 + 1) * P)
-            acc = acc_pool.tile([P, N], F32, name="acc")
+            acc = banks.tile([P, N], F32, name=f"bank{bank}")
             nc.tensor.matmul_mx(
                 out=acc[:],
                 lhsT=codes[c // 2][:, cols].bitcast(FP8X4),
@@ -123,25 +123,30 @@ def tile_list_interp_res_kernel(tc, tab_words, tab_scales, w_words, w_scales, x,
             )
             return acc
 
-        def table_product(g, c):
-            return product(got_codes[g], got_plane[g], c, w_codes[:].bitcast(FP8X4), w_plane)
+        def table_product(g, c, bank):
+            return product(got_codes[g], got_plane[g], c, w_codes[:].bitcast(FP8X4), w_plane, bank)
 
         def skip_product(c):
-            return product(x_codes, x_plane, c, wx_codes[:].bitcast(FP4X4), wx_plane)
+            return product(x_codes, x_plane, c, wx_codes[:].bitcast(FP4X4), wx_plane, 2 + c)
 
         def term_tile(kind, c):
             return keep.tile([P, N], F32, name=f"term_{kind}{c}")
 
         def turn(term, c, first, last):
+            if first:
+                sums[c] = banks.tile([P, NT, P], F32, name=f"bank{c}")
             for a in range(NT):
                 nc.tensor.matmul(
                     out=sums[c][:, a, :],
-                    lhsT=term[:, a * P : (a + 1) * P],
+                    lhsT=term[:, a, :],
                     rhs=ident[:],
                     is_transpose=True,
                     start=first and a == 0,
                     stop=last and a == NT - 1,
                 )
+
+        def by_tile(flat):
+            return flat.rearrange("p (a n) -> p a n", a=NT)
 
         def weight(g, c):
             return iw_cols[:, CHUNKS * g + c : CHUNKS * g + c + 1]
@@ -150,7 +155,7 @@ def tile_list_interp_res_kernel(tc, tab_words, tab_scales, w_words, w_scales, x,
             done = keep.tile([P, len(tiles), P], F32, name=f"done{c}_{tiles.start}")
             rows = slice(tiles.start, tiles.stop)
             cols = slice(c * P, (c + 1) * P)
-            nc.vector.tensor_tensor(done[:], sums[c][:, rows, :], res_sb[:, rows, cols], ADD)
+            nc.vector.tensor_tensor(done[:], sums[c][:, rows, :], res_sb[c // 2][:, rows, (c % 2) * P : (c % 2 + 1) * P], ADD)
             nc.sync.dma_start(out=out_view[:, rows, cols], in_=done[:])
 
         for g in range(2):
@@ -168,8 +173,8 @@ def tile_list_interp_res_kernel(tc, tab_words, tab_scales, w_words, w_scales, x,
                 skip[c] = skips[:, c % 2, :]
                 scalar_copy(out=skip[c], in_=acc[:])
         for c in (0, 1):
-            turn(skip[c], c, True, False)
-        iw_acc = acc_pool.tile([P, N], F32, name="acc")
+            turn(by_tile(skip[c]), c, True, False)
+        iw_acc = banks.tile([P, N], F32, name="bank2")
         nc.tensor.transpose(iw_acc[:, 0:P], iw_rows[:], ident[:])
         scalar_copy(out=iw_cols[:], in_=iw_acc[:, 0 : 2 * CHUNKS])
         for h in range(2):
@@ -178,29 +183,39 @@ def tile_list_interp_res_kernel(tc, tab_words, tab_scales, w_words, w_scales, x,
         terms = {}
 
         def scaled(g, c):
-            acc = table_product(g, c)
+            acc = products[g, c]
             terms[g, c] = term_tile(f"g{g}", c)
             nc.scalar.activation(out=terms[g, c][:], in_=acc[:], func=COPY, scale=weight(g, c))
 
-        def fused(g, c, other):
-            acc = table_product(g, c)
-            terms[g, c] = term_tile(f"g{g}", c)
-            nc.vector.scalar_tensor_tensor(terms[g, c][:], acc[:], weight(g, c), other, MULT, ADD)
+        def fused(g, c, other, term):
+            acc = products[g, c]
+            terms[g, c] = term
+            nc.vector.scalar_tensor_tensor(term, by_tile(acc[:]), weight(g, c), by_tile(other), MULT, ADD)
 
+        products = {}
+        for c in (0, 1):
+            products[0, c] = table_product(0, c, 6 + c)
+        for c in (0, 1):
+            products[1, c] = table_product(1, c, 2 + c)
         for c in (0, 1):
             scaled(0, c)
-        for c in (0, 1):
-            fused(1, c, terms[0, c][:])
         for c in (2, 3):
-            fused(0, c, skip[c])
+            products[0, c] = table_product(0, c, 2 + c)
+        for c in (2, 3):
+            products[1, c] = table_product(1, c, 4 + c)
+        for c in (0, 1):
+            fused(1, c, terms[0, c][:], by_tile(term_tile("g1", c)[:]))
+        fused(0, 2, skip[2], by_tile(term_tile("g0", 2)[:]))
         for c in (2, 3):
             scaled(1, c)
         for c in (0, 1):
             turn(terms[1, c], c, False, True)
-        for c in (2, 3):
-            turn(terms[1, c], c, True, False)
-            turn(terms[0, c], c, False, True)
-        for c in range(CHUNKS - 1):
             finish(c, range(NT))
-        finish(CHUNKS - 1, range(0, NT // 2))
-        finish(CHUNKS - 1, range(NT // 2, NT))
+        fused(0, 3, skip[3], res_sb[0][:, :, 0:P])
+        turn(terms[0, 2], 2, True, False)
+        turn(by_tile(terms[1, 2][:]), 2, False, True)
+        turn(by_tile(terms[1, 3][:]), 3, True, False)
+        turn(terms[0, 3], 3, False, True)
+        finish(2, range(NT))
+        finish(3, range(0, NT // 2))
+        finish(3, range(NT // 2, NT))

@@ -23,6 +23,8 @@ PACK = 4
 HALF = J // 2
 CHUNKS = J // P
 NT = N // P
+SUM_BANKS = (6, 7, 0, 1)
+PRODUCT_BANKS = ((6, 7, 2, 3), (0, 1, 4, 5))
 
 
 def tile_list_interp_res_kernel(tc, tab_words, tab_scales, w_words, w_scales, x, wx_words, wx_scales, iw0, iw1, res, offs, out):
@@ -42,7 +44,9 @@ def tile_list_interp_res_kernel(tc, tab_words, tab_scales, w_words, w_scales, x,
         iw_rows = keep.tile([P, P], F32, name="iw_rows")
         iw_cols = keep.tile([P, 2 * CHUNKS], F32, name="iw_cols")
         x_raw = [keep.tile([P, PACK, HALF], F32, name=f"x_raw{h}") for h in range(2)]
-        x_bf = [keep.tile([P, P, PACK], BF16, name=f"x_bf{c}", align_bytes=64) for c in range(CHUNKS)]
+        x_first = keep.tile([P, HALF, PACK], BF16, name="x_bf0", align_bytes=64)
+        x_bf = [x_first[:, 0:P, :], x_first[:, P:HALF, :]]
+        x_bf += [keep.tile([P, P, PACK], BF16, name=f"x_bf{c}", align_bytes=64)[:] for c in (2, 3)]
         x_codes = [keep.tile([P, HALF], U32, name=f"x_codes{h}", align_bytes=64) for h in range(2)]
         x_plane = [keep.tile([P, HALF], U8, name=f"x_plane{h}", align_bytes=64) for h in range(2)]
         res_sb = [keep.tile([P, NT, HALF], F32, name=f"res_sb{h}") for h in range(2)]
@@ -72,9 +76,9 @@ def tile_list_interp_res_kernel(tc, tab_words, tab_scales, w_words, w_scales, x,
         nc.sync.dma_start(out=x_raw[1][:], in_=x_view[:, :, HALF:J])
         load_plane(nc.sync, wx_plane, wx_scales)
         nc.sync.dma_start(out=tab_codes[:], in_=tab_words[0].rearrange("p t i -> p (t i)").bitcast(I32))
-        nc.sync.dma_start(out=w_codes[:], in_=w_words[0].rearrange("p n i -> p (n i)").bitcast(I32))
         for g, iw in enumerate((iw0, iw1)):
             nc.sync.dma_start(out=iw_rows[CHUNKS * g : CHUNKS * (g + 1), :], in_=iw.rearrange("(c p) -> c p", p=P))
+        nc.sync.dma_start(out=w_codes[:], in_=w_words[0].rearrange("p n i -> p (n i)").bitcast(I32))
         load_plane(nc.sync, w_plane, w_scales)
         for h in range(2):
             nc.sync.dma_start(out=res_sb[h][:], in_=res_view[:, :, h * HALF : (h + 1) * HALF])
@@ -87,7 +91,7 @@ def tile_list_interp_res_kernel(tc, tab_words, tab_scales, w_words, w_scales, x,
             return offsets[:, first : first + HALF // 16]
 
         def gather_plane(g, h):
-            tag = f"got_plane{g}" if h == 0 else f"x_bf{2 + g}"
+            tag = f"got_plane{g}" if h == 0 else f"x_bf{3 * g}"
             got_plane[g][h] = keep.tile([P, HALF], U8, name=tag, align_bytes=64)
             nc.vector.tensor_copy(got_plane[g][h][:], tab_plane[:].bitcast(U8).indirect(list_slice(g, h)))
 
@@ -97,16 +101,15 @@ def tile_list_interp_res_kernel(tc, tab_words, tab_scales, w_words, w_scales, x,
         def interleave(copy, c):
             cols = slice((c % 2) * P, (c % 2 + 1) * P)
             copy(
-                out=x_bf[c][:].rearrange("p (c i) t -> p c t i", i=4),
+                out=x_bf[c].rearrange("p (c i) t -> p c t i", i=4),
                 in_=x_raw[c // 2][:, :, cols].rearrange("p t (c i) -> p c t i", i=4),
             )
 
-        def quantize(c):
-            cols = slice((c % 2) * P, (c % 2 + 1) * P)
+        def quantize(h, cols, rounded):
             nc.vector.quantize_mx(
-                out=x_codes[c // 2][:, cols].bitcast(FP8X4),
-                scales=x_plane[c // 2][:, cols],
-                in_=x_bf[c][:].rearrange("p j t -> p (j t)"),
+                out=x_codes[h][:, cols].bitcast(FP8X4),
+                scales=x_plane[h][:, cols],
+                in_=rounded.rearrange("p j t -> p (j t)"),
             )
 
         def product(codes, plane, c, weights, weights_plane, bank):
@@ -134,7 +137,7 @@ def tile_list_interp_res_kernel(tc, tab_words, tab_scales, w_words, w_scales, x,
 
         def turn(term, c, first, last):
             if first:
-                sums[c] = banks.tile([P, NT, P], F32, name=f"bank{c}")
+                sums[c] = banks.tile([P, NT, P], F32, name=f"bank{SUM_BANKS[c]}")
             for a in range(NT):
                 nc.tensor.matmul(
                     out=sums[c][:, a, :],
@@ -152,28 +155,42 @@ def tile_list_interp_res_kernel(tc, tab_words, tab_scales, w_words, w_scales, x,
             return iw_cols[:, CHUNKS * g + c : CHUNKS * g + c + 1]
 
         def finish(c, tiles):
-            done = keep.tile([P, len(tiles), P], F32, name=f"done{c}_{tiles.start}")
+            if c < 2:
+                done = by_tile(skips[:, c, :])
+            else:
+                done = keep.tile([P, len(tiles), P], F32, name=f"done{c}_{tiles.start}")[:]
             rows = slice(tiles.start, tiles.stop)
             cols = slice(c * P, (c + 1) * P)
-            nc.vector.tensor_tensor(done[:], sums[c][:, rows, :], res_sb[c // 2][:, rows, (c % 2) * P : (c % 2 + 1) * P], ADD)
-            nc.sync.dma_start(out=out_view[:, rows, cols], in_=done[:])
+            nc.vector.tensor_tensor(done, sums[c][:, rows, :], addend[c // 2][:, rows, (c % 2) * P : (c % 2 + 1) * P], ADD)
+            nc.sync.dma_start(out=out_view[:, rows, cols], in_=done)
 
         for g in range(2):
             gather_plane(g, 0)
         for c in range(CHUNKS):
             interleave(scalar_copy, c)
-            quantize(c)
-        for g in range(2):
-            gather_plane(g, 1)
-        skip = {}
-        for h in range(2):
-            skips = keep.tile([P, 2, N], F32, name=f"x_raw{1 - h}")
-            for c in (2 * h, 2 * h + 1):
-                acc = skip_product(c)
-                skip[c] = skips[:, c % 2, :]
-                scalar_copy(out=skip[c], in_=acc[:])
-        for c in (0, 1):
-            turn(by_tile(skip[c]), c, True, False)
+        quantize(0, slice(0, HALF), x_first[:])
+        gather_plane(0, 1)
+        for c in (2, 3):
+            quantize(1, slice((c % 2) * P, (c % 2 + 1) * P), x_bf[c])
+        gather_plane(1, 1)
+        early = keep.tile([P, NT, HALF], F32, name="x_raw1")
+        for pair in range(2):
+            acc = banks.tile([P, 2, HALF], F32, name=f"bank{2 + pair}")
+            for a in (2 * pair, 2 * pair + 1):
+                nc.tensor.matmul_mx(
+                    out=acc[:, a % 2, :],
+                    lhsT=wx_codes[:, a * P // 2 : (a + 1) * P // 2].bitcast(FP4X4),
+                    lhsT_scale=wx_plane[:].bitcast(U8)[:, a * P : (a + 1) * P],
+                    rhs=x_codes[0][:].bitcast(FP8X4),
+                    rhs_scale=x_plane[0][:],
+                    start=True,
+                    stop=True,
+                )
+            scalar_copy(out=early[:, 2 * pair : 2 * pair + 2, :], in_=acc[:])
+        skips = keep.tile([P, 2, N], F32, name="x_raw0")
+        for c in (2, 3):
+            acc = skip_product(c)
+            scalar_copy(out=skips[:, c % 2, :], in_=acc[:])
         iw_acc = banks.tile([P, N], F32, name="bank2")
         nc.tensor.transpose(iw_acc[:, 0:P], iw_rows[:], ident[:])
         scalar_copy(out=iw_cols[:], in_=iw_acc[:, 0 : 2 * CHUNKS])
@@ -192,30 +209,29 @@ def tile_list_interp_res_kernel(tc, tab_words, tab_scales, w_words, w_scales, x,
             terms[g, c] = term
             nc.vector.scalar_tensor_tensor(term, by_tile(acc[:]), weight(g, c), by_tile(other), MULT, ADD)
 
+        joined = keep.tile([P, NT, HALF], F32, name="tab_codes", align_bytes=64)
+        for c in (0, 1):
+            cols = slice(c * P, (c + 1) * P)
+            nc.gpsimd.tensor_tensor(joined[:, :, cols], early[:, :, cols], res_sb[0][:, :, cols], ADD)
+        addend = (joined, res_sb[1])
         products = {}
-        for c in (0, 1):
-            products[0, c] = table_product(0, c, 6 + c)
-        for c in (0, 1):
-            products[1, c] = table_product(1, c, 2 + c)
+        for h in range(2):
+            for g in range(2):
+                for c in (2 * h, 2 * h + 1):
+                    products[g, c] = table_product(g, c, PRODUCT_BANKS[g][c])
         for c in (0, 1):
             scaled(0, c)
-        for c in (2, 3):
-            products[0, c] = table_product(0, c, 2 + c)
-        for c in (2, 3):
-            products[1, c] = table_product(1, c, 4 + c)
         for c in (0, 1):
             fused(1, c, terms[0, c][:], by_tile(term_tile("g1", c)[:]))
-        fused(0, 2, skip[2], by_tile(term_tile("g0", 2)[:]))
         for c in (2, 3):
             scaled(1, c)
         for c in (0, 1):
-            turn(terms[1, c], c, False, True)
+            turn(terms[1, c], c, True, True)
+            fused(0, c + 2, skips[:, c, :], by_tile(term_tile("g0", c + 2)[:]))
             finish(c, range(NT))
-        fused(0, 3, skip[3], res_sb[0][:, :, 0:P])
-        turn(terms[0, 2], 2, True, False)
-        turn(by_tile(terms[1, 2][:]), 2, False, True)
-        turn(by_tile(terms[1, 3][:]), 3, True, False)
-        turn(terms[0, 3], 3, False, True)
+        for c in (2, 3):
+            turn(by_tile(terms[1, c][:]), c, True, False)
+            turn(terms[0, c], c, False, True)
         finish(2, range(NT))
         finish(3, range(0, NT // 2))
         finish(3, range(NT // 2, NT))

@@ -23,7 +23,7 @@ PACK = 4
 HALF = J // 2
 CHUNKS = J // P
 NT = N // P
-SUM_BANKS = (6, 7, 0, 1)
+SUM_BANKS = (6, 4, 2, 7)
 PRODUCT_BANKS = ((6, 7, 2, 3), (0, 1, 4, 5))
 
 
@@ -155,8 +155,10 @@ def tile_list_interp_res_kernel(tc, tab_words, tab_scales, w_words, w_scales, x,
             return iw_cols[:, CHUNKS * g + c : CHUNKS * g + c + 1]
 
         def finish(c, tiles):
-            if c < 2:
-                done = by_tile(skips[:, c, :])
+            if c == 0:
+                done = by_tile(skips[:, 1, :])
+            elif c == 1:
+                done = res_sb[1][:, :, 0:P]
             else:
                 done = keep.tile([P, len(tiles), P], F32, name=f"done{c}_{tiles.start}")[:]
             rows = slice(tiles.start, tiles.stop)
@@ -221,17 +223,21 @@ def tile_list_interp_res_kernel(tc, tab_words, tab_scales, w_words, w_scales, x,
                     products[g, c] = table_product(g, c, PRODUCT_BANKS[g][c])
         for c in (0, 1):
             scaled(0, c)
-        for c in (0, 1):
-            fused(1, c, terms[0, c][:], by_tile(term_tile("g1", c)[:]))
+        scaled(1, 0)
+        fused(0, 2, skips[:, 0, :], by_tile(term_tile("g0", 2)[:]))
+        fused(1, 1, terms[0, 1][:], by_tile(skips[:, 0, :]))
+        fused(0, 3, skips[:, 1, :], by_tile(term_tile("g0", 3)[:]))
         for c in (2, 3):
             scaled(1, c)
-        for c in (0, 1):
-            turn(terms[1, c], c, True, True)
-            fused(0, c + 2, skips[:, c, :], by_tile(term_tile("g0", c + 2)[:]))
-            finish(c, range(NT))
-        for c in (2, 3):
-            turn(by_tile(terms[1, c][:]), c, True, False)
-            turn(terms[0, c], c, False, True)
+        for g in range(2):
+            turn(by_tile(terms[g, 0][:]), 0, g == 0, g == 1)
+        finish(0, range(NT))
+        turn(terms[0, 2], 2, True, False)
+        turn(by_tile(terms[1, 2][:]), 2, False, True)
         finish(2, range(NT))
+        turn(terms[1, 1], 1, True, True)
+        finish(1, range(NT))
+        turn(terms[0, 3], 3, True, False)
+        turn(by_tile(terms[1, 3][:]), 3, False, True)
         finish(3, range(0, NT // 2))
         finish(3, range(NT // 2, NT))

@@ -43,10 +43,10 @@ def tile_list_interp_res_kernel(tc, tab_words, tab_scales, w_words, w_scales, x,
         ident = keep.tile([P, P], F32, name="ident")
         iw_rows = keep.tile([P, P], F32, name="iw_rows")
         iw_cols = keep.tile([P, 2 * CHUNKS], F32, name="iw_cols")
-        x_raw = [keep.tile([P, PACK, HALF], F32, name=f"x_raw{h}") for h in range(2)]
-        x_first = keep.tile([P, HALF, PACK], BF16, name="x_bf0", align_bytes=64)
-        x_bf = [x_first[:, 0:P, :], x_first[:, P:HALF, :]]
-        x_bf += [keep.tile([P, P, PACK], BF16, name=f"x_bf{c}", align_bytes=64)[:] for c in (2, 3)]
+        x_lead = keep.tile([P, PACK, P], F32, name="x_lead")
+        x_rest = keep.tile([P, PACK, J - P], F32, name="x_rest")
+        x_raw = [x_lead[:]] + [x_rest[:, :, c * P : (c + 1) * P] for c in range(CHUNKS - 1)]
+        x_bf = [keep.tile([P, P, PACK], BF16, name=f"x_bf{c}", align_bytes=64)[:] for c in range(CHUNKS)]
         x_codes = [keep.tile([P, HALF], U32, name=f"x_codes{h}", align_bytes=64) for h in range(2)]
         x_plane = [keep.tile([P, HALF], U8, name=f"x_plane{h}", align_bytes=64) for h in range(2)]
         res_sb = [keep.tile([P, NT, HALF], F32, name=f"res_sb{h}") for h in range(2)]
@@ -63,17 +63,18 @@ def tile_list_interp_res_kernel(tc, tab_words, tab_scales, w_words, w_scales, x,
         res_view = res.rearrange("(a p) j -> p a j", p=P)
         out_view = out.rearrange("(a p) j -> p a j", p=P)
 
-        nc.vector.memset(tab_plane[:], 0)
+        nc.vector.memset(tab_plane[:, 0 : T // 8], 0)
+        nc.gpsimd.memset(tab_plane[:, T // 8 : T // 4], 0)
         nc.vector.memset(wx_plane[:], 0)
         nc.vector.memset(w_plane[:], 0)
         nc.gpsimd.memset(iw_rows[:], 0.0)
         make_identity(nc, ident[:])
 
         nc.sync.dma_start(offsets[:], offs)
-        nc.sync.dma_start(out=x_raw[0][:], in_=x_view[:, :, 0:HALF])
-        load_plane(nc.sync, tab_plane, tab_scales)
+        nc.sync.dma_start(out=x_lead[:], in_=x_view[:, :, 0:P])
         nc.sync.dma_start(out=wx_codes[:], in_=wx_words[0].bitcast(I32))
-        nc.sync.dma_start(out=x_raw[1][:], in_=x_view[:, :, HALF:J])
+        load_plane(nc.sync, tab_plane, tab_scales)
+        nc.sync.dma_start(out=x_rest[:], in_=x_view[:, :, P:J])
         load_plane(nc.sync, wx_plane, wx_scales)
         nc.sync.dma_start(out=tab_codes[:], in_=tab_words[0].rearrange("p t i -> p (t i)").bitcast(I32))
         for g, iw in enumerate((iw0, iw1)):
@@ -91,7 +92,7 @@ def tile_list_interp_res_kernel(tc, tab_words, tab_scales, w_words, w_scales, x,
             return offsets[:, first : first + HALF // 16]
 
         def gather_plane(g, h):
-            tag = f"got_plane{g}" if h == 0 else f"x_bf{3 * g}"
+            tag = f"got_plane{g}" if h == 0 else f"x_bf{2 + g}"
             got_plane[g][h] = keep.tile([P, HALF], U8, name=tag, align_bytes=64)
             nc.vector.tensor_copy(got_plane[g][h][:], tab_plane[:].bitcast(U8).indirect(list_slice(g, h)))
 
@@ -99,10 +100,9 @@ def tile_list_interp_res_kernel(tc, tab_words, tab_scales, w_words, w_scales, x,
             nc.vector.tensor_copy(got_codes[g][h][:], tab_codes[:].bitcast(U32).indirect(list_slice(g, h)))
 
         def interleave(copy, c):
-            cols = slice((c % 2) * P, (c % 2 + 1) * P)
             copy(
                 out=x_bf[c].rearrange("p (c i) t -> p c t i", i=4),
-                in_=x_raw[c // 2][:, :, cols].rearrange("p t (c i) -> p c t i", i=4),
+                in_=x_raw[c].rearrange("p t (c i) -> p c t i", i=4),
             )
 
         def quantize(h, cols, rounded):
@@ -168,28 +168,35 @@ def tile_list_interp_res_kernel(tc, tab_words, tab_scales, w_words, w_scales, x,
 
         for g in range(2):
             gather_plane(g, 0)
-        for c in range(CHUNKS):
+        for c in (0, 1):
             interleave(scalar_copy, c)
-        quantize(0, slice(0, HALF), x_first[:])
-        gather_plane(0, 1)
+        quantize(0, slice(0, P), x_bf[0])
         for c in (2, 3):
-            quantize(1, slice((c % 2) * P, (c % 2 + 1) * P), x_bf[c])
-        gather_plane(1, 1)
-        early = keep.tile([P, NT, HALF], F32, name="x_raw1")
-        for pair in range(2):
-            acc = banks.tile([P, 2, HALF], F32, name=f"bank{2 + pair}")
-            for a in (2 * pair, 2 * pair + 1):
+            interleave(nc.vector.tensor_copy, c)
+        for c in (1, 2, 3):
+            quantize(c // 2, slice((c % 2) * P, (c % 2 + 1) * P), x_bf[c])
+        for g in range(2):
+            gather_plane(g, 1)
+        early = keep.tile([P, NT, HALF], F32, name="early")
+        skips = keep.tile([P, 2, N], F32, name="skips")
+
+        def early_skip(c):
+            cols = slice(c * P, (c + 1) * P)
+            acc = banks.tile([P, NT, P], F32, name=f"bank{2 + c}")
+            for a in range(NT):
                 nc.tensor.matmul_mx(
-                    out=acc[:, a % 2, :],
+                    out=acc[:, a, :],
                     lhsT=wx_codes[:, a * P // 2 : (a + 1) * P // 2].bitcast(FP4X4),
                     lhsT_scale=wx_plane[:].bitcast(U8)[:, a * P : (a + 1) * P],
-                    rhs=x_codes[0][:].bitcast(FP8X4),
-                    rhs_scale=x_plane[0][:],
+                    rhs=x_codes[0][:, cols].bitcast(FP8X4),
+                    rhs_scale=x_plane[0][:, cols],
                     start=True,
                     stop=True,
                 )
-            scalar_copy(out=early[:, 2 * pair : 2 * pair + 2, :], in_=acc[:])
-        skips = keep.tile([P, 2, N], F32, name="x_raw0")
+            scalar_copy(out=early[:, :, cols], in_=acc[:])
+
+        for c in (0, 1):
+            early_skip(c)
         for c in (2, 3):
             acc = skip_product(c)
             scalar_copy(out=skips[:, c % 2, :], in_=acc[:])

@@ -23,7 +23,9 @@ PACK = 4
 HALF = J // 2
 CHUNKS = J // P
 NT = N // P
-SUM_BANKS = (6, 4, 2, 7)
+SKIP_BANKS = (2, 3, 4, 5)
+WEIGHT_BANK = 2
+SUM_BANKS = ((6, 6), (7, 7), (0, 0), (4, 2))
 PRODUCT_BANKS = ((6, 7, 2, 3), (0, 1, 4, 5))
 
 
@@ -59,6 +61,9 @@ def tile_list_interp_res_kernel(tc, tab_words, tab_scales, w_words, w_scales, x,
             for r in range(4):
                 queue.dma_start(out=plane[r:P:32, :], in_=rows[r:16:4, :])
 
+        def load_weights(g, iw):
+            nc.sync.dma_start(out=iw_rows[CHUNKS * g : CHUNKS * (g + 1), :], in_=iw.rearrange("(c p) -> c p", p=P))
+
         x_view = x.rearrange("(p t) j -> p t j", t=PACK)
         res_view = res.rearrange("(a p) j -> p a j", p=P)
         out_view = out.rearrange("(a p) j -> p a j", p=P)
@@ -75,10 +80,10 @@ def tile_list_interp_res_kernel(tc, tab_words, tab_scales, w_words, w_scales, x,
         nc.sync.dma_start(out=wx_codes[:], in_=wx_words[0].bitcast(I32))
         load_plane(nc.sync, tab_plane, tab_scales)
         nc.sync.dma_start(out=x_rest[:], in_=x_view[:, :, P:J])
+        load_weights(0, iw0)
         load_plane(nc.sync, wx_plane, wx_scales)
         nc.sync.dma_start(out=tab_codes[:], in_=tab_words[0].rearrange("p t i -> p (t i)").bitcast(I32))
-        for g, iw in enumerate((iw0, iw1)):
-            nc.sync.dma_start(out=iw_rows[CHUNKS * g : CHUNKS * (g + 1), :], in_=iw.rearrange("(c p) -> c p", p=P))
+        load_weights(1, iw1)
         nc.sync.dma_start(out=w_codes[:], in_=w_words[0].rearrange("p n i -> p (n i)").bitcast(I32))
         load_plane(nc.sync, w_plane, w_scales)
         for h in range(2):
@@ -130,41 +135,35 @@ def tile_list_interp_res_kernel(tc, tab_words, tab_scales, w_words, w_scales, x,
             return product(got_codes[g], got_plane[g], c, w_codes[:].bitcast(FP8X4), w_plane, bank)
 
         def skip_product(c):
-            return product(x_codes, x_plane, c, wx_codes[:].bitcast(FP4X4), wx_plane, 2 + c)
-
-        def term_tile(kind, c):
-            return keep.tile([P, N], F32, name=f"term_{kind}{c}")
+            return product(x_codes, x_plane, c, wx_codes[:].bitcast(FP4X4), wx_plane, SKIP_BANKS[c])
 
         def turn(term, c, first, last):
-            if first:
-                sums[c] = banks.tile([P, NT, P], F32, name=f"bank{SUM_BANKS[c]}")
             for a in range(NT):
+                bank = SUM_BANKS[c][a // 2]
+                opens = a == 0 or bank != SUM_BANKS[c][(a - 1) // 2]
+                closes = a == NT - 1 or bank != SUM_BANKS[c][(a + 1) // 2]
+                if first and opens:
+                    sums[bank] = banks.tile([P, NT, P], F32, name=f"bank{bank}")
                 nc.tensor.matmul(
-                    out=sums[c][:, a, :],
-                    lhsT=term[:, a, :],
+                    out=sums[bank][:, a, :],
+                    lhsT=term[:, a * P : (a + 1) * P],
                     rhs=ident[:],
                     is_transpose=True,
-                    start=first and a == 0,
-                    stop=last and a == NT - 1,
+                    start=first and opens,
+                    stop=last and closes,
                 )
-
-        def by_tile(flat):
-            return flat.rearrange("p (a n) -> p a n", a=NT)
 
         def weight(g, c):
             return iw_cols[:, CHUNKS * g + c : CHUNKS * g + c + 1]
 
+        def residual(c):
+            return res_sb[c // 2][:, :, (c % 2) * P : (c % 2 + 1) * P]
+
         def finish(c, tiles):
-            if c == 0:
-                done = by_tile(skips[:, 1, :])
-            elif c == 1:
-                done = res_sb[1][:, :, 0:P]
-            else:
-                done = keep.tile([P, len(tiles), P], F32, name=f"done{c}_{tiles.start}")[:]
+            done = keep.tile([P, len(tiles), P], F32, name=f"done{c}_{tiles.start}")
             rows = slice(tiles.start, tiles.stop)
-            cols = slice(c * P, (c + 1) * P)
-            nc.vector.tensor_tensor(done, sums[c][:, rows, :], addend[c // 2][:, rows, (c % 2) * P : (c % 2 + 1) * P], ADD)
-            nc.sync.dma_start(out=out_view[:, rows, cols], in_=done)
+            nc.vector.tensor_tensor(done[:], sums[SUM_BANKS[c][tiles.start // 2]][:, rows, :], addend[c][:, rows, :], ADD)
+            nc.sync.dma_start(out=out_view[:, rows, c * P : (c + 1) * P], in_=done[:])
 
         for g in range(2):
             gather_plane(g, 0)
@@ -177,74 +176,65 @@ def tile_list_interp_res_kernel(tc, tab_words, tab_scales, w_words, w_scales, x,
             quantize(c // 2, slice((c % 2) * P, (c % 2 + 1) * P), x_bf[c])
         for g in range(2):
             gather_plane(g, 1)
-        early = keep.tile([P, NT, HALF], F32, name="early")
-        skips = keep.tile([P, 2, N], F32, name="skips")
-
-        def early_skip(c):
-            cols = slice(c * P, (c + 1) * P)
-            acc = banks.tile([P, NT, P], F32, name=f"bank{2 + c}")
+        skips = {}
+        for c in range(CHUNKS - 1):
+            cols = slice((c % 2) * P, (c % 2 + 1) * P)
+            acc = banks.tile([P, NT, P], F32, name=f"bank{SKIP_BANKS[c]}")
             for a in range(NT):
                 nc.tensor.matmul_mx(
                     out=acc[:, a, :],
                     lhsT=wx_codes[:, a * P // 2 : (a + 1) * P // 2].bitcast(FP4X4),
                     lhsT_scale=wx_plane[:].bitcast(U8)[:, a * P : (a + 1) * P],
-                    rhs=x_codes[0][:, cols].bitcast(FP8X4),
-                    rhs_scale=x_plane[0][:, cols],
+                    rhs=x_codes[c // 2][:, cols].bitcast(FP8X4),
+                    rhs_scale=x_plane[c // 2][:, cols],
                     start=True,
                     stop=True,
                 )
-            scalar_copy(out=early[:, :, cols], in_=acc[:])
-
-        for c in (0, 1):
-            early_skip(c)
-        for c in (2, 3):
-            acc = skip_product(c)
-            scalar_copy(out=skips[:, c % 2, :], in_=acc[:])
-        iw_acc = banks.tile([P, N], F32, name="bank2")
+            skips[c] = keep.tile([P, NT, P], F32, name=f"skip{c}")
+            scalar_copy(out=skips[c][:], in_=acc[:])
+        acc = skip_product(3)
+        skips[3] = keep.tile([P, N], F32, name="skip3")
+        scalar_copy(out=skips[3][:], in_=acc[:])
+        iw_acc = banks.tile([P, N], F32, name=f"bank{WEIGHT_BANK}")
         nc.tensor.transpose(iw_acc[:, 0:P], iw_rows[:], ident[:])
         scalar_copy(out=iw_cols[:], in_=iw_acc[:, 0 : 2 * CHUNKS])
         for h in range(2):
             for g in range(2):
                 gather_codes(g, h)
+        addend = {3: residual(3)}
+        for c in range(CHUNKS - 1):
+            joined = keep.tile([P, NT, P], F32, name=f"joined{c}")
+            nc.gpsimd.tensor_tensor(joined[:], skips[c][:], residual(c), ADD)
+            addend[c] = joined[:]
+
+        products = {}
         terms = {}
 
         def scaled(g, c):
-            acc = products[g, c]
-            terms[g, c] = term_tile(f"g{g}", c)
-            nc.scalar.activation(out=terms[g, c][:], in_=acc[:], func=COPY, scale=weight(g, c))
+            terms[g, c] = keep.tile([P, N], F32, name=f"term{g}{c}")
+            nc.scalar.activation(out=terms[g, c][:], in_=products[g, c][:], func=COPY, scale=weight(g, c))
 
-        def fused(g, c, other, term):
-            acc = products[g, c]
-            terms[g, c] = term
-            nc.vector.scalar_tensor_tensor(term, by_tile(acc[:]), weight(g, c), by_tile(other), MULT, ADD)
+        def fused(g, c, other, tag):
+            terms[g, c] = keep.tile([P, N], F32, name=tag)
+            nc.vector.scalar_tensor_tensor(terms[g, c][:], products[g, c][:], weight(g, c), other[:], MULT, ADD)
 
-        joined = keep.tile([P, NT, HALF], F32, name="tab_codes", align_bytes=64)
-        for c in (0, 1):
-            cols = slice(c * P, (c + 1) * P)
-            nc.gpsimd.tensor_tensor(joined[:, :, cols], early[:, :, cols], res_sb[0][:, :, cols], ADD)
-        addend = (joined, res_sb[1])
-        products = {}
         for h in range(2):
             for g in range(2):
                 for c in (2 * h, 2 * h + 1):
                     products[g, c] = table_product(g, c, PRODUCT_BANKS[g][c])
-        for c in (0, 1):
-            scaled(0, c)
-        scaled(1, 0)
-        fused(0, 2, skips[:, 0, :], by_tile(term_tile("g0", 2)[:]))
-        fused(1, 1, terms[0, 1][:], by_tile(skips[:, 0, :]))
-        fused(0, 3, skips[:, 1, :], by_tile(term_tile("g0", 3)[:]))
-        for c in (2, 3):
-            scaled(1, c)
+        for g, c in ((0, 0), (0, 1), (1, 0), (0, 2), (1, 2), (1, 3)):
+            scaled(g, c)
+        fused(1, 1, terms[0, 1], "term11")
+        fused(0, 3, skips[3], "term01")
         for g in range(2):
-            turn(by_tile(terms[g, 0][:]), 0, g == 0, g == 1)
+            turn(terms[g, 0], 0, g == 0, g == 1)
         finish(0, range(NT))
-        turn(terms[0, 2], 2, True, False)
-        turn(by_tile(terms[1, 2][:]), 2, False, True)
-        finish(2, range(NT))
         turn(terms[1, 1], 1, True, True)
         finish(1, range(NT))
-        turn(terms[0, 3], 3, True, False)
-        turn(by_tile(terms[1, 3][:]), 3, False, True)
-        finish(3, range(0, NT // 2))
-        finish(3, range(NT // 2, NT))
+        for g in range(2):
+            turn(terms[g, 2], 2, g == 0, g == 1)
+        finish(2, range(NT))
+        for g in range(2):
+            turn(terms[g, 3], 3, g == 0, g == 1)
+        for half in range(2):
+            finish(3, range(2 * half, 2 * half + 2))

@@ -4,7 +4,7 @@ import concourse.mybir as mybir
 from concourse.masks import make_identity
 
 K, L, N, T, J = 512, 512, 512, 2048, 512
-FLOPS = 2 * 3 * K * N * J
+FLOPS = 2 * (2 * K + L) * N * J
 
 F32 = mybir.dt.float32
 BF16 = mybir.dt.bfloat16
@@ -20,13 +20,17 @@ ADD = mybir.AluOpType.add
 
 P = 128
 PACK = 4
+GROUP = 16
+QUADRANT = 32
 HALF = J // 2
 CHUNKS = J // P
-NT = N // P
+LAST = CHUNKS - 1
+TILES = N // P
+
 SKIP_BANKS = (2, 3, 4, 5)
-WEIGHT_BANK = 2
-SUM_BANKS = ((6, 6), (7, 7), (0, 0), (4, 2))
+WEIGHT_BANK = SKIP_BANKS[0]
 PRODUCT_BANKS = ((6, 7, 2, 3), (0, 1, 4, 5))
+SUM_BANKS = ((6, 6), (0, 0), (7, 7), (4, 2))
 
 
 def tile_list_interp_res_kernel(tc, tab_words, tab_scales, w_words, w_scales, x, wx_words, wx_scales, iw0, iw1, res, offs, out):
@@ -35,10 +39,10 @@ def tile_list_interp_res_kernel(tc, tab_words, tab_scales, w_words, w_scales, x,
         keep = ctx.enter_context(tc.tile_pool(name="keep", bufs=1))
         banks = ctx.enter_context(tc.psum_pool(name="banks", bufs=1))
 
-        offsets = keep.tile([P, 2 * J // 16], U16, name="offsets")
-        tab_plane = keep.tile([P, T // 4], I32, name="tab_plane", align_bytes=64)
-        w_plane = keep.tile([P, N // 4], I32, name="w_plane", align_bytes=64)
-        wx_plane = keep.tile([P, N // 4], I32, name="wx_plane", align_bytes=64)
+        offsets = keep.tile([P, 2 * J // GROUP], U16, name="offsets")
+        tab_scale = keep.tile([P, T // 4], I32, name="tab_scale", align_bytes=64)
+        w_scale = keep.tile([P, N // 4], I32, name="w_scale", align_bytes=64)
+        wx_scale = keep.tile([P, N // 4], I32, name="wx_scale", align_bytes=64)
         tab_codes = keep.tile([P, T], I32, name="tab_codes", align_bytes=64)
         w_codes = keep.tile([P, N], I32, name="w_codes", align_bytes=64)
         wx_codes = keep.tile([P, N // 2], I32, name="wx_codes", align_bytes=64)
@@ -50,16 +54,17 @@ def tile_list_interp_res_kernel(tc, tab_words, tab_scales, w_words, w_scales, x,
         x_raw = [x_lead[:]] + [x_rest[:, :, c * P : (c + 1) * P] for c in range(CHUNKS - 1)]
         x_bf = [keep.tile([P, P, PACK], BF16, name=f"x_bf{c}", align_bytes=64)[:] for c in range(CHUNKS)]
         x_codes = [keep.tile([P, HALF], U32, name=f"x_codes{h}", align_bytes=64) for h in range(2)]
-        x_plane = [keep.tile([P, HALF], U8, name=f"x_plane{h}", align_bytes=64) for h in range(2)]
-        res_sb = [keep.tile([P, NT, HALF], F32, name=f"res_sb{h}") for h in range(2)]
+        x_scale = [keep.tile([P, HALF], U8, name=f"x_scale{h}", align_bytes=64) for h in range(2)]
+        res_cols = (slice(0, P), slice(P, HALF), slice(HALF, J))
+        res_sb = [keep.tile([P, TILES, cols.stop - cols.start], F32, name=f"res_sb{cols.start}") for cols in res_cols]
         got_codes = [[keep.tile([P, HALF], U32, name=f"got_codes{g}{h}", align_bytes=64) for h in range(2)] for g in range(2)]
-        got_plane = [[None, None], [None, None]]
+        got_scale = [[None, None], [None, None]]
         sums = {}
 
-        def load_plane(queue, plane, scales):
+        def load_scales(tile, scales):
             rows = scales[0].bitcast(I32)
             for r in range(4):
-                queue.dma_start(out=plane[r:P:32, :], in_=rows[r:16:4, :])
+                nc.sync.dma_start(out=tile[r:P:QUADRANT, :], in_=rows[r:16:4, :])
 
         def load_weights(g, iw):
             nc.sync.dma_start(out=iw_rows[CHUNKS * g : CHUNKS * (g + 1), :], in_=iw.rearrange("(c p) -> c p", p=P))
@@ -68,82 +73,91 @@ def tile_list_interp_res_kernel(tc, tab_words, tab_scales, w_words, w_scales, x,
         res_view = res.rearrange("(a p) j -> p a j", p=P)
         out_view = out.rearrange("(a p) j -> p a j", p=P)
 
-        nc.vector.memset(tab_plane[:, 0 : T // 8], 0)
-        nc.gpsimd.memset(tab_plane[:, T // 8 : T // 4], 0)
-        nc.vector.memset(wx_plane[:], 0)
-        nc.vector.memset(w_plane[:], 0)
+        nc.vector.memset(tab_scale[:, 0 : T // 8], 0)
+        nc.gpsimd.memset(tab_scale[:, T // 8 : T // 4], 0)
+        nc.vector.memset(wx_scale[:], 0)
+        nc.vector.memset(w_scale[:], 0)
         nc.gpsimd.memset(iw_rows[:], 0.0)
         make_identity(nc, ident[:])
 
         nc.sync.dma_start(offsets[:], offs)
         nc.sync.dma_start(out=x_lead[:], in_=x_view[:, :, 0:P])
         nc.sync.dma_start(out=wx_codes[:], in_=wx_words[0].bitcast(I32))
-        load_plane(nc.sync, tab_plane, tab_scales)
+        load_scales(tab_scale, tab_scales)
         nc.sync.dma_start(out=x_rest[:], in_=x_view[:, :, P:J])
         load_weights(0, iw0)
-        load_plane(nc.sync, wx_plane, wx_scales)
+        load_scales(wx_scale, wx_scales)
         nc.sync.dma_start(out=tab_codes[:], in_=tab_words[0].rearrange("p t i -> p (t i)").bitcast(I32))
         load_weights(1, iw1)
         nc.sync.dma_start(out=w_codes[:], in_=w_words[0].rearrange("p n i -> p (n i)").bitcast(I32))
-        load_plane(nc.sync, w_plane, w_scales)
-        for h in range(2):
-            nc.sync.dma_start(out=res_sb[h][:], in_=res_view[:, :, h * HALF : (h + 1) * HALF])
+        load_scales(w_scale, w_scales)
+        for piece, cols in zip(res_sb, res_cols):
+            nc.sync.dma_start(out=piece[:], in_=res_view[:, :, cols])
 
         def scalar_copy(out, in_):
             nc.scalar.activation(out=out, in_=in_, func=COPY)
 
-        def list_slice(g, h):
-            first = (g * J + h * HALF) // 16
-            return offsets[:, first : first + HALF // 16]
+        def in_half(c):
+            return slice((c % 2) * P, (c % 2 + 1) * P)
 
-        def gather_plane(g, h):
-            tag = f"got_plane{g}" if h == 0 else f"x_bf{2 + g}"
-            got_plane[g][h] = keep.tile([P, HALF], U8, name=tag, align_bytes=64)
-            nc.vector.tensor_copy(got_plane[g][h][:], tab_plane[:].bitcast(U8).indirect(list_slice(g, h)))
+        def list_slice(g, h):
+            first = (g * J + h * HALF) // GROUP
+            return offsets[:, first : first + HALF // GROUP]
+
+        def gather_scales(g, h, tag):
+            got_scale[g][h] = keep.tile([P, HALF], U8, name=tag, align_bytes=64)
+            nc.vector.tensor_copy(got_scale[g][h][:], tab_scale[:].bitcast(U8).indirect(list_slice(g, h)))
 
         def gather_codes(g, h):
             nc.vector.tensor_copy(got_codes[g][h][:], tab_codes[:].bitcast(U32).indirect(list_slice(g, h)))
 
         def interleave(copy, c):
             copy(
-                out=x_bf[c].rearrange("p (c i) t -> p c t i", i=4),
-                in_=x_raw[c].rearrange("p t (c i) -> p c t i", i=4),
+                out=x_bf[c].rearrange("p (s i) t -> p s t i", i=4),
+                in_=x_raw[c].rearrange("p t (s i) -> p s t i", i=4),
             )
 
-        def quantize(h, cols, rounded):
+        def quantize(c):
             nc.vector.quantize_mx(
-                out=x_codes[h][:, cols].bitcast(FP8X4),
-                scales=x_plane[h][:, cols],
-                in_=rounded.rearrange("p j t -> p (j t)"),
+                out=x_codes[c // 2][:, in_half(c)].bitcast(FP8X4),
+                scales=x_scale[c // 2][:, in_half(c)],
+                in_=x_bf[c].rearrange("p j t -> p (j t)"),
             )
 
-        def product(codes, plane, c, weights, weights_plane, bank):
-            cols = slice((c % 2) * P, (c % 2 + 1) * P)
+        def product_jn(codes, scale, c, moving, moving_scale, bank):
             acc = banks.tile([P, N], F32, name=f"bank{bank}")
             nc.tensor.matmul_mx(
                 out=acc[:],
-                lhsT=codes[c // 2][:, cols].bitcast(FP8X4),
-                lhsT_scale=plane[c // 2][:, cols],
-                rhs=weights,
-                rhs_scale=weights_plane[:].bitcast(U8),
+                lhsT=codes[c // 2][:, in_half(c)].bitcast(FP8X4),
+                lhsT_scale=scale[c // 2][:, in_half(c)],
+                rhs=moving,
+                rhs_scale=moving_scale[:].bitcast(U8),
                 start=True,
                 stop=True,
             )
             return acc
 
-        def table_product(g, c, bank):
-            return product(got_codes[g], got_plane[g], c, w_codes[:].bitcast(FP8X4), w_plane, bank)
-
-        def skip_product(c):
-            return product(x_codes, x_plane, c, wx_codes[:].bitcast(FP4X4), wx_plane, SKIP_BANKS[c])
+        def skip_product_nj(c):
+            acc = banks.tile([P, TILES, P], F32, name=f"bank{SKIP_BANKS[c]}")
+            for a in range(TILES):
+                nc.tensor.matmul_mx(
+                    out=acc[:, a, :],
+                    lhsT=wx_codes[:, a * P // 2 : (a + 1) * P // 2].bitcast(FP4X4),
+                    lhsT_scale=wx_scale[:].bitcast(U8)[:, a * P : (a + 1) * P],
+                    rhs=x_codes[c // 2][:, in_half(c)].bitcast(FP8X4),
+                    rhs_scale=x_scale[c // 2][:, in_half(c)],
+                    start=True,
+                    stop=True,
+                )
+            return acc
 
         def turn(term, c, first, last):
-            for a in range(NT):
+            for a in range(TILES):
                 bank = SUM_BANKS[c][a // 2]
                 opens = a == 0 or bank != SUM_BANKS[c][(a - 1) // 2]
-                closes = a == NT - 1 or bank != SUM_BANKS[c][(a + 1) // 2]
+                closes = a == TILES - 1 or bank != SUM_BANKS[c][(a + 1) // 2]
                 if first and opens:
-                    sums[bank] = banks.tile([P, NT, P], F32, name=f"bank{bank}")
+                    sums[bank] = banks.tile([P, TILES, P], F32, name=f"bank{bank}")
                 nc.tensor.matmul(
                     out=sums[bank][:, a, :],
                     lhsT=term[:, a * P : (a + 1) * P],
@@ -157,7 +171,7 @@ def tile_list_interp_res_kernel(tc, tab_words, tab_scales, w_words, w_scales, x,
             return iw_cols[:, CHUNKS * g + c : CHUNKS * g + c + 1]
 
         def residual(c):
-            return res_sb[c // 2][:, :, (c % 2) * P : (c % 2 + 1) * P]
+            return res_sb[c][:] if c < 2 else res_sb[2][:, :, in_half(c)]
 
         def finish(c, tiles):
             done = keep.tile([P, len(tiles), P], F32, name=f"done{c}_{tiles.start}")
@@ -166,44 +180,37 @@ def tile_list_interp_res_kernel(tc, tab_words, tab_scales, w_words, w_scales, x,
             nc.sync.dma_start(out=out_view[:, rows, c * P : (c + 1) * P], in_=done[:])
 
         for g in range(2):
-            gather_plane(g, 0)
-        for c in (0, 1):
+            gather_scales(g, 0, f"got_scale{g}")
+        for c in (0, LAST):
             interleave(scalar_copy, c)
-        quantize(0, slice(0, P), x_bf[0])
-        for c in (2, 3):
+        quantize(0)
+        for c in range(1, LAST):
             interleave(nc.vector.tensor_copy, c)
-        for c in (1, 2, 3):
-            quantize(c // 2, slice((c % 2) * P, (c % 2 + 1) * P), x_bf[c])
+        for c in range(1, CHUNKS):
+            quantize(c)
         for g in range(2):
-            gather_plane(g, 1)
+            gather_scales(g, 1, f"x_bf{2 + g}")
+
         skips = {}
-        for c in range(CHUNKS - 1):
-            cols = slice((c % 2) * P, (c % 2 + 1) * P)
-            acc = banks.tile([P, NT, P], F32, name=f"bank{SKIP_BANKS[c]}")
-            for a in range(NT):
-                nc.tensor.matmul_mx(
-                    out=acc[:, a, :],
-                    lhsT=wx_codes[:, a * P // 2 : (a + 1) * P // 2].bitcast(FP4X4),
-                    lhsT_scale=wx_plane[:].bitcast(U8)[:, a * P : (a + 1) * P],
-                    rhs=x_codes[c // 2][:, cols].bitcast(FP8X4),
-                    rhs_scale=x_plane[c // 2][:, cols],
-                    start=True,
-                    stop=True,
-                )
-            skips[c] = keep.tile([P, NT, P], F32, name=f"skip{c}")
+        for c in range(LAST):
+            acc = skip_product_nj(c)
+            skips[c] = keep.tile([P, TILES, P], F32, name=f"skip{c}")
             scalar_copy(out=skips[c][:], in_=acc[:])
-        acc = skip_product(3)
-        skips[3] = keep.tile([P, N], F32, name="skip3")
-        scalar_copy(out=skips[3][:], in_=acc[:])
+        acc = product_jn(x_codes, x_scale, LAST, wx_codes[:].bitcast(FP4X4), wx_scale, SKIP_BANKS[LAST])
+        skips[LAST] = keep.tile([P, N], F32, name=f"skip{LAST}")
+        scalar_copy(out=skips[LAST][:], in_=acc[:])
+
         iw_acc = banks.tile([P, N], F32, name=f"bank{WEIGHT_BANK}")
         nc.tensor.transpose(iw_acc[:, 0:P], iw_rows[:], ident[:])
         scalar_copy(out=iw_cols[:], in_=iw_acc[:, 0 : 2 * CHUNKS])
+
         for h in range(2):
             for g in range(2):
                 gather_codes(g, h)
-        addend = {3: residual(3)}
-        for c in range(CHUNKS - 1):
-            joined = keep.tile([P, NT, P], F32, name=f"joined{c}")
+
+        addend = {LAST: residual(LAST)}
+        for c in range(LAST):
+            joined = keep.tile([P, TILES, P], F32, name=f"joined{c}")
             nc.gpsimd.tensor_tensor(joined[:], skips[c][:], residual(c), ADD)
             addend[c] = joined[:]
 
@@ -218,23 +225,23 @@ def tile_list_interp_res_kernel(tc, tab_words, tab_scales, w_words, w_scales, x,
             terms[g, c] = keep.tile([P, N], F32, name=tag)
             nc.vector.scalar_tensor_tensor(terms[g, c][:], products[g, c][:], weight(g, c), other[:], MULT, ADD)
 
-        for h in range(2):
+        in_gather_order = [(g, c) for h in range(2) for g in range(2) for c in (2 * h, 2 * h + 1)]
+        for g, c in in_gather_order:
+            products[g, c] = product_jn(got_codes[g], got_scale[g], c, w_codes[:].bitcast(FP8X4), w_scale, PRODUCT_BANKS[g][c])
+        on_vector = ((1, 0), (0, LAST))
+        for g, c in in_gather_order:
+            if (g, c) not in on_vector:
+                scaled(g, c)
+        fused(1, 0, terms[0, 0], "term10")
+        fused(0, LAST, skips[LAST], "term00")
+
+        turn(terms[1, 0], 0, True, True)
+        finish(0, range(TILES))
+        for c in range(1, LAST):
             for g in range(2):
-                for c in (2 * h, 2 * h + 1):
-                    products[g, c] = table_product(g, c, PRODUCT_BANKS[g][c])
-        for g, c in ((0, 0), (0, 1), (1, 0), (0, 2), (1, 2), (1, 3)):
-            scaled(g, c)
-        fused(1, 1, terms[0, 1], "term11")
-        fused(0, 3, skips[3], "term01")
+                turn(terms[g, c], c, g == 0, g == 1)
+            finish(c, range(TILES))
         for g in range(2):
-            turn(terms[g, 0], 0, g == 0, g == 1)
-        finish(0, range(NT))
-        turn(terms[1, 1], 1, True, True)
-        finish(1, range(NT))
-        for g in range(2):
-            turn(terms[g, 2], 2, g == 0, g == 1)
-        finish(2, range(NT))
-        for g in range(2):
-            turn(terms[g, 3], 3, g == 0, g == 1)
+            turn(terms[g, LAST], LAST, g == 0, g == 1)
         for half in range(2):
-            finish(3, range(2 * half, 2 * half + 2))
+            finish(LAST, range(2 * half, 2 * half + 2))

@@ -30,7 +30,7 @@ TILES = N // P
 SKIP_BANKS = (2, 3, 4, 5)
 WEIGHT_BANK = SKIP_BANKS[0]
 PRODUCT_BANKS = ((6, 7, 2, 3), (0, 1, 4, 5))
-SUM_BANKS = ((6, 6), (0, 0), (7, 7), (4, 2))
+SUM_BANKS = ((6, 6), (7, 7), (1, 2), (3, 0))
 
 
 def tile_list_interp_res_kernel(tc, tab_words, tab_scales, w_words, w_scales, x, wx_words, wx_scales, iw0, iw1, res, offs, out):
@@ -151,8 +151,8 @@ def tile_list_interp_res_kernel(tc, tab_words, tab_scales, w_words, w_scales, x,
                 )
             return acc
 
-        def turn(term, c, first, last):
-            for a in range(TILES):
+        def turn(term, c, first, last, tiles=range(TILES)):
+            for a in tiles:
                 bank = SUM_BANKS[c][a // 2]
                 opens = a == 0 or bank != SUM_BANKS[c][(a - 1) // 2]
                 closes = a == TILES - 1 or bank != SUM_BANKS[c][(a + 1) // 2]
@@ -228,20 +228,28 @@ def tile_list_interp_res_kernel(tc, tab_words, tab_scales, w_words, w_scales, x,
         in_gather_order = [(g, c) for h in range(2) for g in range(2) for c in (2 * h, 2 * h + 1)]
         for g, c in in_gather_order:
             products[g, c] = product_jn(got_codes[g], got_scale[g], c, w_codes[:].bitcast(FP8X4), w_scale, PRODUCT_BANKS[g][c])
-        on_vector = ((1, 0), (0, LAST))
-        for g, c in in_gather_order:
-            if (g, c) not in on_vector:
+        on_vector = ((1, 0), (0, LAST), (1, 1))
+        for g, c in in_gather_order[:6] + [(1, LAST), (1, 2)]:
+            if (g, c) == (0, LAST):
+                upper = keep.tile([P, N], F32, name="upper")
+                nc.scalar.activation(out=upper[:, N // 2 : N], in_=products[g, c][:, N // 2 : N], func=COPY, scale=weight(g, c))
+            elif (g, c) not in on_vector:
                 scaled(g, c)
         fused(1, 0, terms[0, 0], "term10")
-        fused(0, LAST, skips[LAST], "term00")
+        fused(1, 1, terms[0, 1], "term11")
+        lower = keep.tile([P, N], F32, name="term00")
+        nc.vector.scalar_tensor_tensor(lower[:, 0 : N // 2], products[0, LAST][:, 0 : N // 2], weight(0, LAST), skips[LAST][:, 0 : N // 2], MULT, ADD)
 
-        turn(terms[1, 0], 0, True, True)
-        finish(0, range(TILES))
-        for c in range(1, LAST):
-            for g in range(2):
-                turn(terms[g, c], c, g == 0, g == 1)
+        for c in range(2):
+            turn(terms[1, c], c, True, True)
             finish(c, range(TILES))
-        for g in range(2):
-            turn(terms[g, LAST], LAST, g == 0, g == 1)
+        turn(skips[LAST], LAST, True, False, range(2, 4))
+        turn(upper, LAST, False, False, range(2, 4))
+        turn(terms[0, 2], 2, True, False)
+        turn(lower, LAST, True, False, range(2))
+        turn(terms[1, LAST], LAST, False, True)
         for half in range(2):
             finish(LAST, range(2 * half, 2 * half + 2))
+        turn(terms[1, 2], 2, False, True)
+        for half in range(2):
+            finish(2, range(2 * half, 2 * half + 2))

@@ -30,7 +30,8 @@ TILES = N // P
 SKIP_BANKS = (2, 3, 4, 5)
 WEIGHT_BANK = SKIP_BANKS[0]
 PRODUCT_BANKS = ((6, 7, 2, 3), (0, 1, 4, 5))
-SUM_BANKS = ((6, 6), (7, 7), (1, 2), (3, 0))
+CHUNK_BANKS = (6, 7)
+PAIR_BANKS = (0, 1)
 
 
 def tile_list_interp_res_kernel(tc, tab_words, tab_scales, w_words, w_scales, x, wx_words, wx_scales, iw0, iw1, res, offs, out):
@@ -151,20 +152,18 @@ def tile_list_interp_res_kernel(tc, tab_words, tab_scales, w_words, w_scales, x,
                 )
             return acc
 
-        def turn(term, c, first, last, tiles=range(TILES)):
+        def turn(term, c, tiles, opens=(), closes=()):
             for a in tiles:
-                bank = SUM_BANKS[c][a // 2]
-                opens = a == 0 or bank != SUM_BANKS[c][(a - 1) // 2]
-                closes = a == TILES - 1 or bank != SUM_BANKS[c][(a + 1) // 2]
-                if first and opens:
-                    sums[bank] = banks.tile([P, TILES, P], F32, name=f"bank{bank}")
+                bank = CHUNK_BANKS[c] if c < 2 else PAIR_BANKS[a // 2]
+                if a in opens:
+                    sums[bank] = banks.tile([P, TILES, P] if c < 2 else [P, 2, HALF], F32, name=f"bank{bank}")
                 nc.tensor.matmul(
-                    out=sums[bank][:, a, :],
+                    out=sums[bank][:, a, :] if c < 2 else sums[bank][:, a % 2, in_half(c)],
                     lhsT=term[:, a * P : (a + 1) * P],
                     rhs=ident[:],
                     is_transpose=True,
-                    start=first and opens,
-                    stop=last and closes,
+                    start=a in opens,
+                    stop=a in closes,
                 )
 
         def weight(g, c):
@@ -173,11 +172,10 @@ def tile_list_interp_res_kernel(tc, tab_words, tab_scales, w_words, w_scales, x,
         def residual(c):
             return res_sb[c][:] if c < 2 else res_sb[2][:, :, in_half(c)]
 
-        def finish(c, tiles):
-            done = keep.tile([P, len(tiles), P], F32, name=f"done{c}_{tiles.start}")
-            rows = slice(tiles.start, tiles.stop)
-            nc.vector.tensor_tensor(done[:], sums[SUM_BANKS[c][tiles.start // 2]][:, rows, :], addend[c][:, rows, :], ADD)
-            nc.sync.dma_start(out=out_view[:, rows, c * P : (c + 1) * P], in_=done[:])
+        def finish(total, other, rows, cols):
+            done = keep.tile(list(total.shape), F32, name=f"done{rows.start}_{cols.start}")
+            nc.vector.tensor_tensor(done[:], total, other, ADD)
+            nc.sync.dma_start(out=out_view[:, rows, cols], in_=done[:])
 
         for g in range(2):
             gather_scales(g, 0, f"got_scale{g}")
@@ -208,11 +206,8 @@ def tile_list_interp_res_kernel(tc, tab_words, tab_scales, w_words, w_scales, x,
             for g in range(2):
                 gather_codes(g, h)
 
-        addend = {LAST: residual(LAST)}
         for c in range(LAST):
-            joined = keep.tile([P, TILES, P], F32, name=f"joined{c}")
-            nc.gpsimd.tensor_tensor(joined[:], skips[c][:], residual(c), ADD)
-            addend[c] = joined[:]
+            nc.gpsimd.tensor_tensor(residual(c), skips[c][:], residual(c), ADD)
 
         products = {}
         terms = {}
@@ -229,27 +224,33 @@ def tile_list_interp_res_kernel(tc, tab_words, tab_scales, w_words, w_scales, x,
         for g, c in in_gather_order:
             products[g, c] = product_jn(got_codes[g], got_scale[g], c, w_codes[:].bitcast(FP8X4), w_scale, PRODUCT_BANKS[g][c])
         on_vector = ((1, 0), (0, LAST), (1, 1))
-        for g, c in in_gather_order[:6] + [(1, LAST), (1, 2)]:
+        for g, c in in_gather_order[:6]:
             if (g, c) == (0, LAST):
                 upper = keep.tile([P, N], F32, name="upper")
                 nc.scalar.activation(out=upper[:, N // 2 : N], in_=products[g, c][:, N // 2 : N], func=COPY, scale=weight(g, c))
             elif (g, c) not in on_vector:
                 scaled(g, c)
+        for c in (LAST, 2):
+            terms[1, c] = keep.tile([P, N], F32, name=f"term1{c}")
+        for cols in (slice(0, N // 2), slice(N // 2, N)):
+            for c in (LAST, 2):
+                nc.scalar.activation(out=terms[1, c][:, cols], in_=products[1, c][:, cols], func=COPY, scale=weight(1, c))
         fused(1, 0, terms[0, 0], "term10")
         fused(1, 1, terms[0, 1], "term11")
         lower = keep.tile([P, N], F32, name="term00")
         nc.vector.scalar_tensor_tensor(lower[:, 0 : N // 2], products[0, LAST][:, 0 : N // 2], weight(0, LAST), skips[LAST][:, 0 : N // 2], MULT, ADD)
 
         for c in range(2):
-            turn(terms[1, c], c, True, True)
-            finish(c, range(TILES))
-        turn(skips[LAST], LAST, True, False, range(2, 4))
-        turn(upper, LAST, False, False, range(2, 4))
-        turn(terms[0, 2], 2, True, False)
-        turn(lower, LAST, True, False, range(2))
-        turn(terms[1, LAST], LAST, False, True)
-        for half in range(2):
-            finish(LAST, range(2 * half, 2 * half + 2))
-        turn(terms[1, 2], 2, False, True)
-        for half in range(2):
-            finish(2, range(2 * half, 2 * half + 2))
+            turn(terms[1, c], c, range(TILES), opens=(0,), closes=(TILES - 1,))
+            finish(sums[CHUNK_BANKS[c]][:], residual(c), slice(0, TILES), slice(c * P, (c + 1) * P))
+        turn(terms[0, 2], 2, range(2), opens=(0,))
+        turn(lower, LAST, range(2))
+        turn(terms[1, LAST], LAST, range(2))
+        turn(terms[1, 2], 2, range(2), closes=(1,))
+        turn(skips[LAST], LAST, range(2, 4), opens=(2,))
+        turn(upper, LAST, range(2, 4))
+        turn(terms[0, 2], 2, range(2, 4))
+        turn(terms[1, LAST], LAST, range(2, 4))
+        turn(terms[1, 2], 2, range(2, 4), closes=(3,))
+        for a in range(TILES):
+            finish(sums[PAIR_BANKS[a // 2]][:, a % 2 : a % 2 + 1, :], res_sb[2][:, a : a + 1, :], slice(a, a + 1), slice(HALF, J))

@@ -30,8 +30,7 @@ TILES = N // P
 SKIP_BANKS = (2, 3, 4, 5)
 WEIGHT_BANK = SKIP_BANKS[0]
 PRODUCT_BANKS = ((6, 7, 2, 3), (0, 1, 4, 5))
-CHUNK_BANKS = (6, 7)
-PAIR_BANKS = (0, 1)
+SUM_BANKS = ((6, 7), (0, 1))
 
 
 def tile_list_interp_res_kernel(tc, tab_words, tab_scales, w_words, w_scales, x, wx_words, wx_scales, iw0, iw1, res, offs, out):
@@ -56,8 +55,8 @@ def tile_list_interp_res_kernel(tc, tab_words, tab_scales, w_words, w_scales, x,
         x_bf = [keep.tile([P, P, PACK], BF16, name=f"x_bf{c}", align_bytes=64)[:] for c in range(CHUNKS)]
         x_codes = [keep.tile([P, HALF], U32, name=f"x_codes{h}", align_bytes=64) for h in range(2)]
         x_scale = [keep.tile([P, HALF], U8, name=f"x_scale{h}", align_bytes=64) for h in range(2)]
-        res_cols = (slice(0, P), slice(P, HALF), slice(HALF, J))
-        res_sb = [keep.tile([P, TILES, cols.stop - cols.start], F32, name=f"res_sb{cols.start}") for cols in res_cols]
+        res_parts = ((0, slice(0, 2)), (0, slice(2, TILES)), (1, slice(0, TILES)))
+        res_sb = [keep.tile([P, rows.stop - rows.start, HALF], F32, name=f"res_sb{h}{rows.start}") for h, rows in res_parts]
         got_codes = [[keep.tile([P, HALF], U32, name=f"got_codes{g}{h}", align_bytes=64) for h in range(2)] for g in range(2)]
         got_scale = [[None, None], [None, None]]
         sums = {}
@@ -92,8 +91,8 @@ def tile_list_interp_res_kernel(tc, tab_words, tab_scales, w_words, w_scales, x,
         load_weights(1, iw1)
         nc.sync.dma_start(out=w_codes[:], in_=w_words[0].rearrange("p n i -> p (n i)").bitcast(I32))
         load_scales(w_scale, w_scales)
-        for piece, cols in zip(res_sb, res_cols):
-            nc.sync.dma_start(out=piece[:], in_=res_view[:, :, cols])
+        for piece, (h, rows) in zip(res_sb, res_parts):
+            nc.sync.dma_start(out=piece[:], in_=res_view[:, rows, h * HALF : (h + 1) * HALF])
 
         def scalar_copy(out, in_):
             nc.scalar.activation(out=out, in_=in_, func=COPY)
@@ -154,11 +153,11 @@ def tile_list_interp_res_kernel(tc, tab_words, tab_scales, w_words, w_scales, x,
 
         def turn(term, c, tiles, opens=(), closes=()):
             for a in tiles:
-                bank = CHUNK_BANKS[c] if c < 2 else PAIR_BANKS[a // 2]
+                bank = SUM_BANKS[c // 2][a // 2]
                 if a in opens:
-                    sums[bank] = banks.tile([P, TILES, P] if c < 2 else [P, 2, HALF], F32, name=f"bank{bank}")
+                    sums[bank] = banks.tile([P, 2, HALF], F32, name=f"bank{bank}")
                 nc.tensor.matmul(
-                    out=sums[bank][:, a, :] if c < 2 else sums[bank][:, a % 2, in_half(c)],
+                    out=sums[bank][:, a % 2, in_half(c)],
                     lhsT=term[:, a * P : (a + 1) * P],
                     rhs=ident[:],
                     is_transpose=True,
@@ -169,13 +168,11 @@ def tile_list_interp_res_kernel(tc, tab_words, tab_scales, w_words, w_scales, x,
         def weight(g, c):
             return iw_cols[:, CHUNKS * g + c : CHUNKS * g + c + 1]
 
-        def residual(c):
-            return res_sb[c][:] if c < 2 else res_sb[2][:, :, in_half(c)]
-
-        def finish(total, other, rows, cols):
-            done = keep.tile(list(total.shape), F32, name=f"done{rows.start}_{cols.start}")
-            nc.vector.tensor_tensor(done[:], total, other, ADD)
-            nc.sync.dma_start(out=out_view[:, rows, cols], in_=done[:])
+        def finish(h, a):
+            done = keep.tile([P, HALF], F32, name=f"done{h}{a}")
+            addend = res_sb[a // 2][:, a % 2, :] if h == 0 else res_sb[2][:, a, :]
+            nc.vector.tensor_tensor(done[:], sums[SUM_BANKS[h][a // 2]][:, a % 2, :], addend, ADD)
+            nc.sync.dma_start(out=out_view[:, a, h * HALF : (h + 1) * HALF], in_=done[:])
 
         for g in range(2):
             gather_scales(g, 0, f"got_scale{g}")
@@ -190,10 +187,10 @@ def tile_list_interp_res_kernel(tc, tab_words, tab_scales, w_words, w_scales, x,
             gather_scales(g, 1, f"x_bf{2 + g}")
 
         skips = {}
+        skip_nj = keep.tile([P, TILES, LAST * P], F32, name="skip_nj")
         for c in range(LAST):
             acc = skip_product_nj(c)
-            skips[c] = keep.tile([P, TILES, P], F32, name=f"skip{c}")
-            scalar_copy(out=skips[c][:], in_=acc[:])
+            scalar_copy(out=skip_nj[:, :, c * P : (c + 1) * P], in_=acc[:])
         acc = product_jn(x_codes, x_scale, LAST, wx_codes[:].bitcast(FP4X4), wx_scale, SKIP_BANKS[LAST])
         skips[LAST] = keep.tile([P, N], F32, name=f"skip{LAST}")
         scalar_copy(out=skips[LAST][:], in_=acc[:])
@@ -206,8 +203,9 @@ def tile_list_interp_res_kernel(tc, tab_words, tab_scales, w_words, w_scales, x,
             for g in range(2):
                 gather_codes(g, h)
 
-        for c in range(LAST):
-            nc.gpsimd.tensor_tensor(residual(c), skips[c][:], residual(c), ADD)
+        for pair in range(2):
+            nc.gpsimd.tensor_tensor(res_sb[pair][:], skip_nj[:, 2 * pair : 2 * pair + 2, 0:HALF], res_sb[pair][:], ADD)
+        nc.gpsimd.tensor_tensor(res_sb[2][:, :, 0:P], skip_nj[:, :, HALF : HALF + P], res_sb[2][:, :, 0:P], ADD)
 
         products = {}
         terms = {}
@@ -240,9 +238,10 @@ def tile_list_interp_res_kernel(tc, tab_words, tab_scales, w_words, w_scales, x,
         lower = keep.tile([P, N], F32, name="term00")
         nc.vector.scalar_tensor_tensor(lower[:, 0 : N // 2], products[0, LAST][:, 0 : N // 2], weight(0, LAST), skips[LAST][:, 0 : N // 2], MULT, ADD)
 
-        for c in range(2):
-            turn(terms[1, c], c, range(TILES), opens=(0,), closes=(TILES - 1,))
-            finish(sums[CHUNK_BANKS[c]][:], residual(c), slice(0, TILES), slice(c * P, (c + 1) * P))
+        turn(terms[1, 0], 0, range(TILES), opens=(0, 2))
+        turn(terms[1, 1], 1, range(TILES), closes=(1, 3))
+        for a in range(TILES):
+            finish(0, a)
         turn(terms[0, 2], 2, range(2), opens=(0,))
         turn(lower, LAST, range(2))
         turn(terms[1, LAST], LAST, range(2))
@@ -253,4 +252,4 @@ def tile_list_interp_res_kernel(tc, tab_words, tab_scales, w_words, w_scales, x,
         turn(terms[1, LAST], LAST, range(2, 4))
         turn(terms[1, 2], 2, range(2, 4), closes=(3,))
         for a in range(TILES):
-            finish(sums[PAIR_BANKS[a // 2]][:, a % 2 : a % 2 + 1, :], res_sb[2][:, a : a + 1, :], slice(a, a + 1), slice(HALF, J))
+            finish(1, a)

@@ -26,6 +26,8 @@ HALF = J // 2
 CHUNKS = J // P
 LAST = CHUNKS - 1
 TILES = N // P
+PAIRS = (range(0, 2), range(2, 4))
+PAIR_COLS = (slice(0, N // 2), slice(N // 2, N))
 
 SKIP_BANKS = (2, 3, 4, 5)
 WEIGHT_BANK = SKIP_BANKS[0]
@@ -101,8 +103,8 @@ def tile_list_interp_res_kernel(tc, tab_words, tab_scales, w_words, w_scales, x,
             return slice((c % 2) * P, (c % 2 + 1) * P)
 
         def list_slice(g, h):
-            first = (g * J + h * HALF) // GROUP
-            return offsets[:, first : first + HALF // GROUP]
+            column = (g * J + h * HALF) // GROUP
+            return offsets[:, column : column + HALF // GROUP]
 
         def gather_scales(g, h, tag):
             got_scale[g][h] = keep.tile([P, HALF], U8, name=tag, align_bytes=64)
@@ -186,14 +188,13 @@ def tile_list_interp_res_kernel(tc, tab_words, tab_scales, w_words, w_scales, x,
         for g in range(2):
             gather_scales(g, 1, f"x_bf{2 + g}")
 
-        skips = {}
         skip_nj = keep.tile([P, TILES, LAST * P], F32, name="skip_nj")
         for c in range(LAST):
             acc = skip_product_nj(c)
             scalar_copy(out=skip_nj[:, :, c * P : (c + 1) * P], in_=acc[:])
         acc = product_jn(x_codes, x_scale, LAST, wx_codes[:].bitcast(FP4X4), wx_scale, SKIP_BANKS[LAST])
-        skips[LAST] = keep.tile([P, N], F32, name=f"skip{LAST}")
-        scalar_copy(out=skips[LAST][:], in_=acc[:])
+        skip_jn = keep.tile([P, N], F32, name=f"skip{LAST}")
+        scalar_copy(out=skip_jn[:], in_=acc[:])
 
         iw_acc = banks.tile([P, N], F32, name=f"bank{WEIGHT_BANK}")
         nc.tensor.transpose(iw_acc[:, 0:P], iw_rows[:], ident[:])
@@ -208,48 +209,51 @@ def tile_list_interp_res_kernel(tc, tab_words, tab_scales, w_words, w_scales, x,
         nc.gpsimd.tensor_tensor(res_sb[2][:, :, 0:P], skip_nj[:, :, HALF : HALF + P], res_sb[2][:, :, 0:P], ADD)
 
         products = {}
+        for h in range(2):
+            for g in range(2):
+                for c in (2 * h, 2 * h + 1):
+                    products[g, c] = product_jn(got_codes[g], got_scale[g], c, w_codes[:].bitcast(FP8X4), w_scale, PRODUCT_BANKS[g][c])
+
+        def scaled(term, g, c, cols):
+            nc.scalar.activation(out=term[:, cols], in_=products[g, c][:, cols], func=COPY, scale=weight(g, c))
+
+        def fused(term, g, c, cols, other):
+            nc.vector.scalar_tensor_tensor(term[:, cols], products[g, c][:, cols], weight(g, c), other[:, cols], MULT, ADD)
+
         terms = {}
-
-        def scaled(g, c):
-            terms[g, c] = keep.tile([P, N], F32, name=f"term{g}{c}")
-            nc.scalar.activation(out=terms[g, c][:], in_=products[g, c][:], func=COPY, scale=weight(g, c))
-
-        def fused(g, c, other, tag):
-            terms[g, c] = keep.tile([P, N], F32, name=tag)
-            nc.vector.scalar_tensor_tensor(terms[g, c][:], products[g, c][:], weight(g, c), other[:], MULT, ADD)
-
-        in_gather_order = [(g, c) for h in range(2) for g in range(2) for c in (2 * h, 2 * h + 1)]
-        for g, c in in_gather_order:
-            products[g, c] = product_jn(got_codes[g], got_scale[g], c, w_codes[:].bitcast(FP8X4), w_scale, PRODUCT_BANKS[g][c])
-        on_vector = ((1, 0), (0, LAST), (1, 1))
-        for g, c in in_gather_order[:6]:
-            if (g, c) == (0, LAST):
-                upper = keep.tile([P, N], F32, name="upper")
-                nc.scalar.activation(out=upper[:, N // 2 : N], in_=products[g, c][:, N // 2 : N], func=COPY, scale=weight(g, c))
-            elif (g, c) not in on_vector:
-                scaled(g, c)
+        for c in range(LAST):
+            terms[0, c] = keep.tile([P, N], F32, name=f"term0{c}")
+            scaled(terms[0, c], 0, c, slice(0, N))
+        upper = keep.tile([P, N], F32, name="upper")
+        scaled(upper, 0, LAST, PAIR_COLS[1])
         for c in (LAST, 2):
             terms[1, c] = keep.tile([P, N], F32, name=f"term1{c}")
-        for cols in (slice(0, N // 2), slice(N // 2, N)):
+        for cols in PAIR_COLS:
             for c in (LAST, 2):
-                nc.scalar.activation(out=terms[1, c][:, cols], in_=products[1, c][:, cols], func=COPY, scale=weight(1, c))
-        fused(1, 0, terms[0, 0], "term10")
-        fused(1, 1, terms[0, 1], "term11")
-        lower = keep.tile([P, N], F32, name="term00")
-        nc.vector.scalar_tensor_tensor(lower[:, 0 : N // 2], products[0, LAST][:, 0 : N // 2], weight(0, LAST), skips[LAST][:, 0 : N // 2], MULT, ADD)
+                scaled(terms[1, c], 1, c, cols)
 
-        turn(terms[1, 0], 0, range(TILES), opens=(0, 2))
-        turn(terms[1, 1], 1, range(TILES), closes=(1, 3))
+        both = [keep.tile([P, N], F32, name=f"term1{c}") for c in range(2)]
+        for cols in PAIR_COLS:
+            for c in range(2):
+                fused(both[c], 1, c, cols, terms[0, c])
+        lower = keep.tile([P, N], F32, name="term00")
+        fused(lower, 0, LAST, PAIR_COLS[0], skip_jn)
+
+        for tiles in PAIRS:
+            turn(both[0], 0, tiles, opens=(tiles[0],))
+            turn(both[1], 1, tiles, closes=(tiles[-1],))
         for a in range(TILES):
             finish(0, a)
-        turn(terms[0, 2], 2, range(2), opens=(0,))
-        turn(lower, LAST, range(2))
-        turn(terms[1, LAST], LAST, range(2))
-        turn(terms[1, 2], 2, range(2), closes=(1,))
-        turn(skips[LAST], LAST, range(2, 4), opens=(2,))
-        turn(upper, LAST, range(2, 4))
-        turn(terms[0, 2], 2, range(2, 4))
-        turn(terms[1, LAST], LAST, range(2, 4))
-        turn(terms[1, 2], 2, range(2, 4), closes=(3,))
+
+        first, second = PAIRS
+        turn(terms[0, 2], 2, first, opens=(first[0],))
+        turn(lower, LAST, first)
+        turn(terms[1, LAST], LAST, first)
+        turn(terms[1, 2], 2, first, closes=(first[-1],))
+        turn(skip_jn, LAST, second, opens=(second[0],))
+        turn(upper, LAST, second)
+        turn(terms[0, 2], 2, second)
+        turn(terms[1, LAST], LAST, second)
+        turn(terms[1, 2], 2, second, closes=(second[-1],))
         for a in range(TILES):
             finish(1, a)

@@ -79,11 +79,12 @@ def tile_list_interp_res_kernel(tc, tab_words, tab_scales, w_words, w_scales, x,
         nc.gpsimd.memset(tab_scale[:, T // 8 : T // 4], 0)
         nc.vector.memset(wx_scale[:], 0)
         nc.vector.memset(w_scale[:], 0)
-        nc.gpsimd.memset(iw_rows[:], 0.0)
-        make_identity(nc, ident[:])
+        nc.vector.memset(iw_rows[:], 0.0)
+        nc.vector.memset(ident[:], 0.0)
+        make_identity(nc, ident[:], nomemset=True)
 
-        nc.sync.dma_start(offsets[:], offs)
         nc.sync.dma_start(out=x_lead[:], in_=x_view[:, :, 0:P])
+        nc.sync.dma_start(offsets[:], offs)
         nc.sync.dma_start(out=wx_codes[:], in_=wx_words[0].bitcast(I32))
         load_scales(tab_scale, tab_scales)
         nc.sync.dma_start(out=x_rest[:], in_=x_view[:, :, P:J])

@@ -32,7 +32,7 @@ PAIR_COLS = (slice(0, N // 2), slice(N // 2, N))
 SKIP_BANKS = (2, 3, 4, 5)
 WEIGHT_BANK = SKIP_BANKS[0]
 PRODUCT_BANKS = ((6, 7, 2, 3), (0, 1, 4, 5))
-SUM_BANKS = ((6, 7), (0, 1))
+SUM_BANKS = ((6, 6, 7, 7), (0, 0, 1, 2))
 
 
 def tile_list_interp_res_kernel(tc, tab_words, tab_scales, w_words, w_scales, x, wx_words, wx_scales, iw0, iw1, res, offs, out):
@@ -156,7 +156,7 @@ def tile_list_interp_res_kernel(tc, tab_words, tab_scales, w_words, w_scales, x,
 
         def turn(term, c, tiles, opens=(), closes=()):
             for a in tiles:
-                bank = SUM_BANKS[c // 2][a // 2]
+                bank = SUM_BANKS[c // 2][a]
                 if a in opens:
                     sums[bank] = banks.tile([P, 2, HALF], F32, name=f"bank{bank}")
                 nc.tensor.matmul(
@@ -174,7 +174,7 @@ def tile_list_interp_res_kernel(tc, tab_words, tab_scales, w_words, w_scales, x,
         def finish(h, a):
             done = keep.tile([P, HALF], F32, name=f"done{h}{a}")
             addend = res_sb[a // 2][:, a % 2, :] if h == 0 else res_sb[2][:, a, :]
-            nc.vector.tensor_tensor(done[:], sums[SUM_BANKS[h][a // 2]][:, a % 2, :], addend, ADD)
+            nc.vector.tensor_tensor(done[:], sums[SUM_BANKS[h][a]][:, a % 2, :], addend, ADD)
             nc.sync.dma_start(out=out_view[:, a, h * HALF : (h + 1) * HALF], in_=done[:])
 
         for g in range(2):
@@ -187,7 +187,7 @@ def tile_list_interp_res_kernel(tc, tab_words, tab_scales, w_words, w_scales, x,
         for c in range(1, CHUNKS):
             quantize(c)
         for g in range(2):
-            gather_scales(g, 1, f"x_bf{2 + g}")
+            gather_scales(g, 1, f"x_bf{1 + g}")
 
         skip_nj = keep.tile([P, TILES, LAST * P], F32, name="skip_nj")
         for c in range(LAST):
@@ -226,7 +226,7 @@ def tile_list_interp_res_kernel(tc, tab_words, tab_scales, w_words, w_scales, x,
             terms[0, c] = keep.tile([P, N], F32, name=f"term0{c}")
             scaled(terms[0, c], 0, c, slice(0, N))
         upper = keep.tile([P, N], F32, name="upper")
-        scaled(upper, 0, LAST, PAIR_COLS[1])
+        scaled(upper, 0, LAST, slice(P, N))
         for c in (LAST, 2):
             terms[1, c] = keep.tile([P, N], F32, name=f"term1{c}")
         for cols in PAIR_COLS:
@@ -238,7 +238,7 @@ def tile_list_interp_res_kernel(tc, tab_words, tab_scales, w_words, w_scales, x,
             for c in range(2):
                 fused(both[c], 1, c, cols, terms[0, c])
         lower = keep.tile([P, N], F32, name="term00")
-        fused(lower, 0, LAST, PAIR_COLS[0], skip_jn)
+        fused(lower, 0, LAST, slice(0, P), skip_jn)
 
         for tiles in PAIRS:
             turn(both[0], 0, tiles, opens=(tiles[0],))
@@ -248,13 +248,15 @@ def tile_list_interp_res_kernel(tc, tab_words, tab_scales, w_words, w_scales, x,
 
         first, second = PAIRS
         turn(terms[0, 2], 2, first, opens=(first[0],))
-        turn(lower, LAST, first)
+        turn(skip_jn, LAST, first[1:])
+        turn(upper, LAST, first[1:])
+        turn(lower, LAST, first[:1])
         turn(terms[1, LAST], LAST, first)
         turn(terms[1, 2], 2, first, closes=(first[-1],))
-        turn(skip_jn, LAST, second, opens=(second[0],))
+        turn(skip_jn, LAST, second, opens=second)
         turn(upper, LAST, second)
         turn(terms[0, 2], 2, second)
         turn(terms[1, LAST], LAST, second)
-        turn(terms[1, 2], 2, second, closes=(second[-1],))
+        turn(terms[1, 2], 2, second, closes=second)
         for a in range(TILES):
             finish(1, a)

@@ -60,7 +60,7 @@ def tile_list_interp_res_kernel(tc, tab_words, tab_scales, w_words, w_scales, x,
         res_parts = ((0, slice(0, 2)), (0, slice(2, TILES)), (1, slice(0, TILES)))
         res_sb = [keep.tile([P, rows.stop - rows.start, HALF], F32, name=f"res_sb{h}{rows.start}") for h, rows in res_parts]
         got_codes = [[keep.tile([P, HALF], U32, name=f"got_codes{g}{h}", align_bytes=64) for h in range(2)] for g in range(2)]
-        got_scale = [[None, None], [None, None]]
+        got_scale = [None, None]
         sums = {}
 
         def load_scales(tile, scales):
@@ -107,9 +107,11 @@ def tile_list_interp_res_kernel(tc, tab_words, tab_scales, w_words, w_scales, x,
             column = (g * J + h * HALF) // GROUP
             return offsets[:, column : column + HALF // GROUP]
 
-        def gather_scales(g, h, tag):
-            got_scale[g][h] = keep.tile([P, HALF], U8, name=tag, align_bytes=64)
-            nc.vector.tensor_copy(got_scale[g][h][:], tab_scale[:].bitcast(U8).indirect(list_slice(g, h)))
+        def gather_scales(g, tag):
+            got = keep.tile([P, J], U8, name=tag, align_bytes=64)
+            entries = offsets[:, g * J // GROUP : (g + 1) * J // GROUP]
+            nc.vector.tensor_copy(got[:], tab_scale[:].bitcast(U8).indirect(entries))
+            got_scale[g] = [got[:, 0:HALF], got[:, HALF:J]]
 
         def gather_codes(g, h):
             nc.vector.tensor_copy(got_codes[g][h][:], tab_codes[:].bitcast(U32).indirect(list_slice(g, h)))
@@ -177,8 +179,7 @@ def tile_list_interp_res_kernel(tc, tab_words, tab_scales, w_words, w_scales, x,
             nc.vector.tensor_tensor(done[:], sums[SUM_BANKS[h][a]][:, a % 2, :], addend, ADD)
             nc.sync.dma_start(out=out_view[:, a, h * HALF : (h + 1) * HALF], in_=done[:])
 
-        for g in range(2):
-            gather_scales(g, 0, f"got_scale{g}")
+        gather_scales(0, "got_scale0")
         for c in (0, LAST):
             interleave(scalar_copy, c)
         quantize(0)
@@ -186,8 +187,7 @@ def tile_list_interp_res_kernel(tc, tab_words, tab_scales, w_words, w_scales, x,
             interleave(nc.vector.tensor_copy, c)
         for c in range(1, CHUNKS):
             quantize(c)
-        for g in range(2):
-            gather_scales(g, 1, f"x_bf{1 + g}")
+        gather_scales(1, "x_bf1")
 
         skip_nj = keep.tile([P, TILES, LAST * P], F32, name="skip_nj")
         for c in range(LAST):

@@ -57,7 +57,7 @@ def tile_list_interp_res_kernel(tc, tab_words, tab_scales, w_words, w_scales, x,
         x_bf = [keep.tile([P, P, PACK], BF16, name=f"x_bf{c}", align_bytes=64)[:] for c in range(CHUNKS)]
         x_codes = [keep.tile([P, HALF], U32, name=f"x_codes{h}", align_bytes=64) for h in range(2)]
         x_scale = [keep.tile([P, HALF], U8, name=f"x_scale{h}", align_bytes=64) for h in range(2)]
-        res_parts = ((0, slice(0, 2)), (0, slice(2, TILES)), (1, slice(0, TILES)))
+        res_parts = ((1, slice(0, 2)), (0, slice(0, 2)), (1, slice(2, TILES)), (0, slice(2, TILES)))
         res_sb = [keep.tile([P, rows.stop - rows.start, HALF], F32, name=f"res_sb{h}{rows.start}") for h, rows in res_parts]
         got_codes = [[keep.tile([P, HALF], U32, name=f"got_codes{g}{h}", align_bytes=64) for h in range(2)] for g in range(2)]
         got_scale = [None, None]
@@ -175,7 +175,7 @@ def tile_list_interp_res_kernel(tc, tab_words, tab_scales, w_words, w_scales, x,
 
         def finish(h, a):
             done = keep.tile([P, HALF], F32, name=f"done{h}{a}")
-            addend = res_sb[a // 2][:, a % 2, :] if h == 0 else res_sb[2][:, a, :]
+            addend = (res_sb[1 + 2 * (a // 2)] if h == 0 else addends[a // 2])[:, a % 2, :]
             nc.vector.tensor_tensor(done[:], sums[SUM_BANKS[h][a]][:, a % 2, :], addend, ADD)
             nc.sync.dma_start(out=out_view[:, a, h * HALF : (h + 1) * HALF], in_=done[:])
 
@@ -189,13 +189,14 @@ def tile_list_interp_res_kernel(tc, tab_words, tab_scales, w_words, w_scales, x,
             quantize(c)
         gather_scales(1, "x_bf1")
 
-        skip_nj = keep.tile([P, TILES, LAST * P], F32, name="skip_nj")
-        for c in range(LAST):
+        skip_jn = [keep.tile([P, N], F32, name=f"skip{c}") for c in range(2)]
+        for c in range(2):
+            acc = product_jn(x_codes, x_scale, c, wx_codes[:].bitcast(FP4X4), wx_scale, SKIP_BANKS[c])
+            scalar_copy(out=skip_jn[c][:], in_=acc[:])
+        skip_nj = keep.tile([P, TILES, HALF], F32, name="skip_nj")
+        for c in range(2, CHUNKS):
             acc = skip_product_nj(c)
-            scalar_copy(out=skip_nj[:, :, c * P : (c + 1) * P], in_=acc[:])
-        acc = product_jn(x_codes, x_scale, LAST, wx_codes[:].bitcast(FP4X4), wx_scale, SKIP_BANKS[LAST])
-        skip_jn = keep.tile([P, N], F32, name=f"skip{LAST}")
-        scalar_copy(out=skip_jn[:], in_=acc[:])
+            scalar_copy(out=skip_nj[:, :, in_half(c)], in_=acc[:])
 
         iw_acc = banks.tile([P, N], F32, name=f"bank{WEIGHT_BANK}")
         nc.tensor.transpose(iw_acc[:, 0:P], iw_rows[:], ident[:])
@@ -205,9 +206,9 @@ def tile_list_interp_res_kernel(tc, tab_words, tab_scales, w_words, w_scales, x,
             for g in range(2):
                 gather_codes(g, h)
 
+        addends = [keep.tile([P, 2, HALF], F32, name="tab_codes", align_bytes=64), res_sb[2]]
         for pair in range(2):
-            nc.gpsimd.tensor_tensor(res_sb[pair][:], skip_nj[:, 2 * pair : 2 * pair + 2, 0:HALF], res_sb[pair][:], ADD)
-        nc.gpsimd.tensor_tensor(res_sb[2][:, :, 0:P], skip_nj[:, :, HALF : HALF + P], res_sb[2][:, :, 0:P], ADD)
+            nc.gpsimd.tensor_tensor(addends[pair][:], skip_nj[:, 2 * pair : 2 * pair + 2, :], res_sb[2 * pair][:], ADD)
 
         products = {}
         for h in range(2):
@@ -222,11 +223,9 @@ def tile_list_interp_res_kernel(tc, tab_words, tab_scales, w_words, w_scales, x,
             nc.vector.scalar_tensor_tensor(term[:, cols], products[g, c][:, cols], weight(g, c), other[:, cols], MULT, ADD)
 
         terms = {}
-        for c in range(LAST):
+        for c in range(CHUNKS):
             terms[0, c] = keep.tile([P, N], F32, name=f"term0{c}")
             scaled(terms[0, c], 0, c, slice(0, N))
-        upper = keep.tile([P, N], F32, name="upper")
-        scaled(upper, 0, LAST, slice(P, N))
         for c in (LAST, 2):
             terms[1, c] = keep.tile([P, N], F32, name=f"term1{c}")
         for cols in PAIR_COLS:
@@ -237,25 +236,23 @@ def tile_list_interp_res_kernel(tc, tab_words, tab_scales, w_words, w_scales, x,
         for cols in PAIR_COLS:
             for c in range(2):
                 fused(both[c], 1, c, cols, terms[0, c])
-        lower = keep.tile([P, N], F32, name="term00")
-        fused(lower, 0, LAST, slice(0, P), skip_jn)
 
         for tiles in PAIRS:
-            turn(both[0], 0, tiles, opens=(tiles[0],))
+            turn(skip_jn[0], 0, tiles, opens=(tiles[0],))
+            turn(skip_jn[1], 1, tiles)
+        for tiles in PAIRS:
+            turn(both[0], 0, tiles)
             turn(both[1], 1, tiles, closes=(tiles[-1],))
         for a in range(TILES):
             finish(0, a)
 
         first, second = PAIRS
         turn(terms[0, 2], 2, first, opens=(first[0],))
-        turn(skip_jn, LAST, first[1:])
-        turn(upper, LAST, first[1:])
-        turn(lower, LAST, first[:1])
+        turn(terms[0, LAST], LAST, first)
         turn(terms[1, LAST], LAST, first)
         turn(terms[1, 2], 2, first, closes=(first[-1],))
-        turn(skip_jn, LAST, second, opens=second)
-        turn(upper, LAST, second)
-        turn(terms[0, 2], 2, second)
+        turn(terms[0, 2], 2, second, opens=second)
+        turn(terms[0, LAST], LAST, second)
         turn(terms[1, LAST], LAST, second)
         turn(terms[1, 2], 2, second, closes=second)
         for a in range(TILES):

@@ -51,16 +51,18 @@ def tile_list_interp_res_kernel(tc, tab_words, tab_scales, w_words, w_scales, x,
         ident = keep.tile([P, P], F32, name="ident")
         iw_rows = keep.tile([P, P], F32, name="iw_rows")
         iw_cols = keep.tile([P, 2 * CHUNKS], F32, name="iw_cols")
-        x_lead = keep.tile([P, PACK, P], F32, name="x_lead")
-        x_rest = keep.tile([P, PACK, J - P], F32, name="x_rest")
-        x_raw = [x_lead[:]] + [x_rest[:, :, c * P : (c + 1) * P] for c in range(CHUNKS - 1)]
-        x_bf = [keep.tile([P, P, PACK], BF16, name=f"x_bf{c}", align_bytes=64)[:] for c in range(CHUNKS)]
+        x_early = [keep.tile([P, PACK, P], F32, name=f"x_early{c}") for c in range(2)]
+        x_late = keep.tile([P, PACK, HALF], F32, name="x_late", align_bytes=64)
+        x_raw = [t[:] for t in x_early] + [x_late[:, :, c * P : (c + 1) * P] for c in range(2)]
+        x_pair = keep.tile([P, HALF, PACK], BF16, name="x_pair", align_bytes=64)
+        x_bf = [x_pair[:, 0:P, :], x_pair[:, P:HALF, :]]
+        x_bf = x_bf + [keep.tile([P, P, PACK], BF16, name=f"x_bf{c}", align_bytes=64)[:] for c in range(2, CHUNKS)]
         x_codes = [keep.tile([P, HALF], U32, name=f"x_codes{h}", align_bytes=64) for h in range(2)]
         x_scale = [keep.tile([P, HALF], U8, name=f"x_scale{h}", align_bytes=64) for h in range(2)]
-        res_parts = ((1, slice(0, 2)), (0, slice(0, 2)), (1, slice(2, TILES)), (0, slice(2, TILES)))
+        res_parts = ((0, slice(0, 2)), (0, slice(2, TILES)), (1, slice(0, TILES)))
         res_sb = [keep.tile([P, rows.stop - rows.start, HALF], F32, name=f"res_sb{h}{rows.start}") for h, rows in res_parts]
         got_codes = [[keep.tile([P, HALF], U32, name=f"got_codes{g}{h}", align_bytes=64) for h in range(2)] for g in range(2)]
-        got_scale = [None, None]
+        got_scale = [[None, None], [None, None]]
         sums = {}
 
         def load_scales(tile, scales):
@@ -69,29 +71,29 @@ def tile_list_interp_res_kernel(tc, tab_words, tab_scales, w_words, w_scales, x,
                 nc.sync.dma_start(out=tile[r:P:QUADRANT, :], in_=rows[r:16:4, :])
 
         def load_weights(g, iw):
-            nc.sync.dma_start(out=iw_rows[CHUNKS * g : CHUNKS * (g + 1), :], in_=iw.rearrange("(c p) -> c p", p=P))
+            nc.gpsimd.dma_start(out=iw_rows[CHUNKS * g : CHUNKS * (g + 1), :], in_=iw.rearrange("(c p) -> c p", p=P))
 
         x_view = x.rearrange("(p t) j -> p t j", t=PACK)
         res_view = res.rearrange("(a p) j -> p a j", p=P)
         out_view = out.rearrange("(a p) j -> p a j", p=P)
 
-        nc.vector.memset(tab_scale[:, 0 : T // 8], 0)
-        nc.gpsimd.memset(tab_scale[:, T // 8 : T // 4], 0)
+        nc.gpsimd.memset(tab_scale[:], 0)
+        nc.vector.memset(iw_rows[:], 0.0)
         nc.vector.memset(wx_scale[:], 0)
         nc.vector.memset(w_scale[:], 0)
-        nc.vector.memset(iw_rows[:], 0.0)
         nc.vector.memset(ident[:], 0.0)
+        load_weights(0, iw0)
+        load_weights(1, iw1)
         make_identity(nc, ident[:], nomemset=True)
 
-        nc.sync.dma_start(out=x_lead[:], in_=x_view[:, :, 0:P])
+        nc.sync.dma_start(out=x_early[0][:], in_=x_view[:, :, 0:P])
         nc.sync.dma_start(offsets[:], offs)
-        nc.sync.dma_start(out=wx_codes[:], in_=wx_words[0].bitcast(I32))
         load_scales(tab_scale, tab_scales)
-        nc.sync.dma_start(out=x_rest[:], in_=x_view[:, :, P:J])
-        load_weights(0, iw0)
+        nc.sync.dma_start(out=x_early[1][:], in_=x_view[:, :, P:HALF])
+        nc.sync.dma_start(out=x_late[:], in_=x_view[:, :, HALF:J])
+        nc.sync.dma_start(out=wx_codes[:], in_=wx_words[0].bitcast(I32))
         load_scales(wx_scale, wx_scales)
         nc.sync.dma_start(out=tab_codes[:], in_=tab_words[0].rearrange("p t i -> p (t i)").bitcast(I32))
-        load_weights(1, iw1)
         nc.sync.dma_start(out=w_codes[:], in_=w_words[0].rearrange("p n i -> p (n i)").bitcast(I32))
         load_scales(w_scale, w_scales)
         for piece, (h, rows) in zip(res_sb, res_parts):
@@ -107,11 +109,12 @@ def tile_list_interp_res_kernel(tc, tab_words, tab_scales, w_words, w_scales, x,
             column = (g * J + h * HALF) // GROUP
             return offsets[:, column : column + HALF // GROUP]
 
-        def gather_scales(g, tag):
-            got = keep.tile([P, J], U8, name=tag, align_bytes=64)
-            entries = offsets[:, g * J // GROUP : (g + 1) * J // GROUP]
+        def gather_scales(first, count, tag):
+            got = keep.tile([P, count * HALF], U8, name=tag, align_bytes=64)
+            entries = offsets[:, first * HALF // GROUP : (first + count) * HALF // GROUP]
             nc.vector.tensor_copy(got[:], tab_scale[:].bitcast(U8).indirect(entries))
-            got_scale[g] = [got[:, 0:HALF], got[:, HALF:J]]
+            for i in range(count):
+                got_scale[(first + i) // 2][(first + i) % 2] = got[:, i * HALF : (i + 1) * HALF]
 
         def gather_codes(g, h):
             nc.vector.tensor_copy(got_codes[g][h][:], tab_codes[:].bitcast(U32).indirect(list_slice(g, h)))
@@ -175,28 +178,27 @@ def tile_list_interp_res_kernel(tc, tab_words, tab_scales, w_words, w_scales, x,
 
         def finish(h, a):
             done = keep.tile([P, HALF], F32, name=f"done{h}{a}")
-            addend = (res_sb[1 + 2 * (a // 2)] if h == 0 else addends[a // 2])[:, a % 2, :]
+            addend = res_sb[a // 2][:, a % 2, :] if h == 0 else res_sb[2][:, a, :]
             nc.vector.tensor_tensor(done[:], sums[SUM_BANKS[h][a]][:, a % 2, :], addend, ADD)
             nc.sync.dma_start(out=out_view[:, a, h * HALF : (h + 1) * HALF], in_=done[:])
 
-        gather_scales(0, "got_scale0")
-        for c in (0, LAST):
-            interleave(scalar_copy, c)
-        quantize(0)
-        for c in range(1, LAST):
-            interleave(nc.vector.tensor_copy, c)
-        for c in range(1, CHUNKS):
-            quantize(c)
-        gather_scales(1, "x_bf1")
-
-        skip_jn = [keep.tile([P, N], F32, name=f"skip{c}") for c in range(2)]
+        gather_scales(0, 2, "got_scale")
         for c in range(2):
-            acc = product_jn(x_codes, x_scale, c, wx_codes[:].bitcast(FP4X4), wx_scale, SKIP_BANKS[c])
-            scalar_copy(out=skip_jn[c][:], in_=acc[:])
-        skip_nj = keep.tile([P, TILES, HALF], F32, name="skip_nj")
-        for c in range(2, CHUNKS):
+            interleave(scalar_copy, c)
+        nc.vector.quantize_mx(out=x_codes[0][:].bitcast(FP8X4), scales=x_scale[0][:], in_=x_pair[:].rearrange("p j t -> p (j t)"))
+        interleave(scalar_copy, LAST)
+        interleave(nc.vector.tensor_copy, 2)
+        quantize(LAST)
+        quantize(2)
+        gather_scales(2, 2, "x_late")
+
+        skip_nj = keep.tile([P, TILES, LAST * P], F32, name="skip_nj")
+        for c in range(LAST):
             acc = skip_product_nj(c)
-            scalar_copy(out=skip_nj[:, :, in_half(c)], in_=acc[:])
+            scalar_copy(out=skip_nj[:, :, c * P : (c + 1) * P], in_=acc[:])
+        acc = product_jn(x_codes, x_scale, LAST, wx_codes[:].bitcast(FP4X4), wx_scale, SKIP_BANKS[LAST])
+        skip_jn = keep.tile([P, N], F32, name=f"skip{LAST}")
+        scalar_copy(out=skip_jn[:], in_=acc[:])
 
         iw_acc = banks.tile([P, N], F32, name=f"bank{WEIGHT_BANK}")
         nc.tensor.transpose(iw_acc[:, 0:P], iw_rows[:], ident[:])
@@ -206,9 +208,9 @@ def tile_list_interp_res_kernel(tc, tab_words, tab_scales, w_words, w_scales, x,
             for g in range(2):
                 gather_codes(g, h)
 
-        addends = [keep.tile([P, 2, HALF], F32, name="tab_codes", align_bytes=64), res_sb[2]]
         for pair in range(2):
-            nc.gpsimd.tensor_tensor(addends[pair][:], skip_nj[:, 2 * pair : 2 * pair + 2, :], res_sb[2 * pair][:], ADD)
+            nc.gpsimd.tensor_tensor(res_sb[pair][:], skip_nj[:, 2 * pair : 2 * pair + 2, 0:HALF], res_sb[pair][:], ADD)
+        nc.gpsimd.tensor_tensor(res_sb[2][:, :, 0:P], skip_nj[:, :, HALF : HALF + P], res_sb[2][:, :, 0:P], ADD)
 
         products = {}
         for h in range(2):
@@ -223,9 +225,11 @@ def tile_list_interp_res_kernel(tc, tab_words, tab_scales, w_words, w_scales, x,
             nc.vector.scalar_tensor_tensor(term[:, cols], products[g, c][:, cols], weight(g, c), other[:, cols], MULT, ADD)
 
         terms = {}
-        for c in range(CHUNKS):
+        for c in range(LAST):
             terms[0, c] = keep.tile([P, N], F32, name=f"term0{c}")
             scaled(terms[0, c], 0, c, slice(0, N))
+        upper = keep.tile([P, N], F32, name="upper")
+        scaled(upper, 0, LAST, slice(P, N))
         for c in (LAST, 2):
             terms[1, c] = keep.tile([P, N], F32, name=f"term1{c}")
         for cols in PAIR_COLS:
@@ -236,23 +240,25 @@ def tile_list_interp_res_kernel(tc, tab_words, tab_scales, w_words, w_scales, x,
         for cols in PAIR_COLS:
             for c in range(2):
                 fused(both[c], 1, c, cols, terms[0, c])
+        lower = keep.tile([P, N], F32, name="term00")
+        fused(lower, 0, LAST, slice(0, P), skip_jn)
 
         for tiles in PAIRS:
-            turn(skip_jn[0], 0, tiles, opens=(tiles[0],))
-            turn(skip_jn[1], 1, tiles)
-        for tiles in PAIRS:
-            turn(both[0], 0, tiles)
+            turn(both[0], 0, tiles, opens=(tiles[0],))
             turn(both[1], 1, tiles, closes=(tiles[-1],))
         for a in range(TILES):
             finish(0, a)
 
         first, second = PAIRS
         turn(terms[0, 2], 2, first, opens=(first[0],))
-        turn(terms[0, LAST], LAST, first)
+        turn(skip_jn, LAST, first[1:])
+        turn(upper, LAST, first[1:])
+        turn(lower, LAST, first[:1])
         turn(terms[1, LAST], LAST, first)
         turn(terms[1, 2], 2, first, closes=(first[-1],))
-        turn(terms[0, 2], 2, second, opens=second)
-        turn(terms[0, LAST], LAST, second)
+        turn(skip_jn, LAST, second, opens=second)
+        turn(upper, LAST, second)
+        turn(terms[0, 2], 2, second)
         turn(terms[1, LAST], LAST, second)
         turn(terms[1, 2], 2, second, closes=second)
         for a in range(TILES):

@@ -50,7 +50,7 @@ def tile_list_interp_res_kernel(tc, tab_words, tab_scales, w_words, w_scales, x,
         wx_codes = keep.tile([P, N // 2], I32, name="wx_codes", align_bytes=64)
         ident = keep.tile([P, P], F32, name="ident")
         iw_rows = keep.tile([P, P], F32, name="iw_rows")
-        iw_cols = keep.tile([P, 2 * CHUNKS], F32, name="iw_cols")
+        iw_cols = [keep.tile([P, CHUNKS], F32, name=f"iw_cols{g}") for g in range(2)]
         x_early = [keep.tile([P, PACK, P], F32, name=f"x_early{c}") for c in range(2)]
         x_late = keep.tile([P, PACK, HALF], F32, name="x_late", align_bytes=64)
         x_raw = [t[:] for t in x_early] + [x_late[:, :, c * P : (c + 1) * P] for c in range(2)]
@@ -70,20 +70,16 @@ def tile_list_interp_res_kernel(tc, tab_words, tab_scales, w_words, w_scales, x,
             for r in range(4):
                 nc.sync.dma_start(out=tile[r:P:QUADRANT, :], in_=rows[r:16:4, :])
 
-        def load_weights(g, iw):
-            nc.gpsimd.dma_start(out=iw_rows[CHUNKS * g : CHUNKS * (g + 1), :], in_=iw.rearrange("(c p) -> c p", p=P))
-
         x_view = x.rearrange("(p t) j -> p t j", t=PACK)
         res_view = res.rearrange("(a p) j -> p a j", p=P)
         out_view = out.rearrange("(a p) j -> p a j", p=P)
 
-        nc.gpsimd.memset(tab_scale[:], 0)
-        nc.vector.memset(iw_rows[:], 0.0)
+        nc.vector.memset(tab_scale[:, 0 : T // 8], 0)
+        nc.gpsimd.memset(tab_scale[:, T // 8 : T // 4], 0)
         nc.vector.memset(wx_scale[:], 0)
         nc.vector.memset(w_scale[:], 0)
+        nc.vector.memset(iw_rows[:], 0.0)
         nc.vector.memset(ident[:], 0.0)
-        load_weights(0, iw0)
-        load_weights(1, iw1)
         make_identity(nc, ident[:], nomemset=True)
 
         nc.sync.dma_start(out=x_early[0][:], in_=x_view[:, :, 0:P])
@@ -94,10 +90,14 @@ def tile_list_interp_res_kernel(tc, tab_words, tab_scales, w_words, w_scales, x,
         nc.sync.dma_start(out=wx_codes[:], in_=wx_words[0].bitcast(I32))
         load_scales(wx_scale, wx_scales)
         nc.sync.dma_start(out=tab_codes[:], in_=tab_words[0].rearrange("p t i -> p (t i)").bitcast(I32))
+        nc.sync.dma_start(out=iw_rows[0:CHUNKS, :], in_=iw0.rearrange("(c p) -> c p", p=P))
         nc.sync.dma_start(out=w_codes[:], in_=w_words[0].rearrange("p n i -> p (n i)").bitcast(I32))
         load_scales(w_scale, w_scales)
-        for piece, (h, rows) in zip(res_sb, res_parts):
-            nc.sync.dma_start(out=piece[:], in_=res_view[:, rows, h * HALF : (h + 1) * HALF])
+        for i, (h, rows) in enumerate(res_parts):
+            nc.sync.dma_start(out=res_sb[i][:], in_=res_view[:, rows, h * HALF : (h + 1) * HALF])
+            if i == 0:
+                with nc.allow_non_contiguous_dma(reason="one weight a partition and chunk"):
+                    nc.sync.dma_start(out=iw_cols[1][:], in_=iw1.rearrange("(c p) -> p c", p=P))
 
         def scalar_copy(out, in_):
             nc.scalar.activation(out=out, in_=in_, func=COPY)
@@ -174,7 +174,7 @@ def tile_list_interp_res_kernel(tc, tab_words, tab_scales, w_words, w_scales, x,
                 )
 
         def weight(g, c):
-            return iw_cols[:, CHUNKS * g + c : CHUNKS * g + c + 1]
+            return iw_cols[g][:, c : c + 1]
 
         def finish(h, a):
             done = keep.tile([P, HALF], F32, name=f"done{h}{a}")
@@ -202,7 +202,7 @@ def tile_list_interp_res_kernel(tc, tab_words, tab_scales, w_words, w_scales, x,
 
         iw_acc = banks.tile([P, N], F32, name=f"bank{WEIGHT_BANK}")
         nc.tensor.transpose(iw_acc[:, 0:P], iw_rows[:], ident[:])
-        scalar_copy(out=iw_cols[:], in_=iw_acc[:, 0 : 2 * CHUNKS])
+        scalar_copy(out=iw_cols[0][:], in_=iw_acc[:, 0:CHUNKS])
 
         for h in range(2):
             for g in range(2):

@@ -51,18 +51,16 @@ def tile_list_interp_res_kernel(tc, tab_words, tab_scales, w_words, w_scales, x,
         ident = keep.tile([P, P], F32, name="ident")
         iw_rows = keep.tile([P, P], F32, name="iw_rows")
         iw_cols = [keep.tile([P, CHUNKS], F32, name=f"iw_cols{g}") for g in range(2)]
-        x_early = [keep.tile([P, PACK, P], F32, name=f"x_early{c}") for c in range(2)]
-        x_late = keep.tile([P, PACK, HALF], F32, name="x_late", align_bytes=64)
-        x_raw = [t[:] for t in x_early] + [x_late[:, :, c * P : (c + 1) * P] for c in range(2)]
-        x_pair = keep.tile([P, HALF, PACK], BF16, name="x_pair", align_bytes=64)
-        x_bf = [x_pair[:, 0:P, :], x_pair[:, P:HALF, :]]
-        x_bf = x_bf + [keep.tile([P, P, PACK], BF16, name=f"x_bf{c}", align_bytes=64)[:] for c in range(2, CHUNKS)]
+        x_lead = keep.tile([P, PACK, P], F32, name="x_lead")
+        x_rest = keep.tile([P, PACK, J - P], F32, name="x_rest")
+        x_raw = [x_lead[:]] + [x_rest[:, :, c * P : (c + 1) * P] for c in range(CHUNKS - 1)]
+        x_bf = [keep.tile([P, P, PACK], BF16, name=f"x_bf{c}", align_bytes=64)[:] for c in range(CHUNKS)]
         x_codes = [keep.tile([P, HALF], U32, name=f"x_codes{h}", align_bytes=64) for h in range(2)]
         x_scale = [keep.tile([P, HALF], U8, name=f"x_scale{h}", align_bytes=64) for h in range(2)]
         res_parts = ((0, slice(0, 2)), (0, slice(2, TILES)), (1, slice(0, TILES)))
         res_sb = [keep.tile([P, rows.stop - rows.start, HALF], F32, name=f"res_sb{h}{rows.start}") for h, rows in res_parts]
         got_codes = [[keep.tile([P, HALF], U32, name=f"got_codes{g}{h}", align_bytes=64) for h in range(2)] for g in range(2)]
-        got_scale = [[None, None], [None, None]]
+        got_scale = []
         sums = {}
 
         def load_scales(tile, scales):
@@ -82,11 +80,10 @@ def tile_list_interp_res_kernel(tc, tab_words, tab_scales, w_words, w_scales, x,
         nc.vector.memset(ident[:], 0.0)
         make_identity(nc, ident[:], nomemset=True)
 
-        nc.sync.dma_start(out=x_early[0][:], in_=x_view[:, :, 0:P])
+        nc.sync.dma_start(out=x_lead[:], in_=x_view[:, :, 0:P])
         nc.sync.dma_start(offsets[:], offs)
         load_scales(tab_scale, tab_scales)
-        nc.sync.dma_start(out=x_early[1][:], in_=x_view[:, :, P:HALF])
-        nc.sync.dma_start(out=x_late[:], in_=x_view[:, :, HALF:J])
+        nc.sync.dma_start(out=x_rest[:], in_=x_view[:, :, P:J])
         nc.sync.dma_start(out=wx_codes[:], in_=wx_words[0].bitcast(I32))
         load_scales(wx_scale, wx_scales)
         nc.sync.dma_start(out=tab_codes[:], in_=tab_words[0].rearrange("p t i -> p (t i)").bitcast(I32))
@@ -109,12 +106,12 @@ def tile_list_interp_res_kernel(tc, tab_words, tab_scales, w_words, w_scales, x,
             column = (g * J + h * HALF) // GROUP
             return offsets[:, column : column + HALF // GROUP]
 
-        def gather_scales(first, count, tag):
-            got = keep.tile([P, count * HALF], U8, name=tag, align_bytes=64)
-            entries = offsets[:, first * HALF // GROUP : (first + count) * HALF // GROUP]
+        def gather_scales(count, tag):
+            first = len(got_scale)
+            got = keep.tile([P, count * P], U8, name=tag, align_bytes=64)
+            entries = offsets[:, first * P // GROUP : (first + count) * P // GROUP]
             nc.vector.tensor_copy(got[:], tab_scale[:].bitcast(U8).indirect(entries))
-            for i in range(count):
-                got_scale[(first + i) // 2][(first + i) % 2] = got[:, i * HALF : (i + 1) * HALF]
+            got_scale.extend(got[:, i * P : (i + 1) * P] for i in range(count))
 
         def gather_codes(g, h):
             nc.vector.tensor_copy(got_codes[g][h][:], tab_codes[:].bitcast(U32).indirect(list_slice(g, h)))
@@ -132,12 +129,12 @@ def tile_list_interp_res_kernel(tc, tab_words, tab_scales, w_words, w_scales, x,
                 in_=x_bf[c].rearrange("p j t -> p (j t)"),
             )
 
-        def product_jn(codes, scale, c, moving, moving_scale, bank):
+        def product_jn(codes, scale, moving, moving_scale, bank):
             acc = banks.tile([P, N], F32, name=f"bank{bank}")
             nc.tensor.matmul_mx(
                 out=acc[:],
-                lhsT=codes[c // 2][:, in_half(c)].bitcast(FP8X4),
-                lhsT_scale=scale[c // 2][:, in_half(c)],
+                lhsT=codes.bitcast(FP8X4),
+                lhsT_scale=scale,
                 rhs=moving,
                 rhs_scale=moving_scale[:].bitcast(U8),
                 start=True,
@@ -182,21 +179,21 @@ def tile_list_interp_res_kernel(tc, tab_words, tab_scales, w_words, w_scales, x,
             nc.vector.tensor_tensor(done[:], sums[SUM_BANKS[h][a]][:, a % 2, :], addend, ADD)
             nc.sync.dma_start(out=out_view[:, a, h * HALF : (h + 1) * HALF], in_=done[:])
 
-        gather_scales(0, 2, "got_scale")
-        for c in range(2):
+        gather_scales(5, "got_scale")
+        for c in (0, LAST):
             interleave(scalar_copy, c)
-        nc.vector.quantize_mx(out=x_codes[0][:].bitcast(FP8X4), scales=x_scale[0][:], in_=x_pair[:].rearrange("p j t -> p (j t)"))
-        interleave(scalar_copy, LAST)
-        interleave(nc.vector.tensor_copy, 2)
-        quantize(LAST)
-        quantize(2)
-        gather_scales(2, 2, "x_late")
+        quantize(0)
+        for c in range(1, LAST):
+            interleave(nc.vector.tensor_copy, c)
+        for c in range(1, CHUNKS):
+            quantize(c)
+        gather_scales(3, "x_bf1")
 
         skip_nj = keep.tile([P, TILES, LAST * P], F32, name="skip_nj")
         for c in range(LAST):
             acc = skip_product_nj(c)
             scalar_copy(out=skip_nj[:, :, c * P : (c + 1) * P], in_=acc[:])
-        acc = product_jn(x_codes, x_scale, LAST, wx_codes[:].bitcast(FP4X4), wx_scale, SKIP_BANKS[LAST])
+        acc = product_jn(x_codes[1][:, in_half(LAST)], x_scale[1][:, in_half(LAST)], wx_codes[:].bitcast(FP4X4), wx_scale, SKIP_BANKS[LAST])
         skip_jn = keep.tile([P, N], F32, name=f"skip{LAST}")
         scalar_copy(out=skip_jn[:], in_=acc[:])
 
@@ -216,7 +213,7 @@ def tile_list_interp_res_kernel(tc, tab_words, tab_scales, w_words, w_scales, x,
         for h in range(2):
             for g in range(2):
                 for c in (2 * h, 2 * h + 1):
-                    products[g, c] = product_jn(got_codes[g], got_scale[g], c, w_codes[:].bitcast(FP8X4), w_scale, PRODUCT_BANKS[g][c])
+                    products[g, c] = product_jn(got_codes[g][h][:, in_half(c)], got_scale[CHUNKS * g + c], w_codes[:].bitcast(FP8X4), w_scale, PRODUCT_BANKS[g][c])
 
         def scaled(term, g, c, cols):
             nc.scalar.activation(out=term[:, cols], in_=products[g, c][:, cols], func=COPY, scale=weight(g, c))

@@ -52,7 +52,7 @@ def tile_list_interp_res_kernel(tc, tab_words, tab_scales, w_words, w_scales, x,
         iw_rows = keep.tile([P, P], F32, name="iw_rows")
         iw_cols = [keep.tile([P, CHUNKS], F32, name=f"iw_cols{g}") for g in range(2)]
         x_lead = keep.tile([P, PACK, P], F32, name="x_lead")
-        x_rest = keep.tile([P, PACK, J - P], F32, name="x_rest")
+        x_rest = keep.tile([P, PACK, J - P], F32, name="x_rest", align_bytes=64)
         x_raw = [x_lead[:]] + [x_rest[:, :, c * P : (c + 1) * P] for c in range(CHUNKS - 1)]
         x_bf = [keep.tile([P, P, PACK], BF16, name=f"x_bf{c}", align_bytes=64)[:] for c in range(CHUNKS)]
         x_codes = [keep.tile([P, HALF], U32, name=f"x_codes{h}", align_bytes=64) for h in range(2)]
@@ -180,14 +180,13 @@ def tile_list_interp_res_kernel(tc, tab_words, tab_scales, w_words, w_scales, x,
             nc.sync.dma_start(out=out_view[:, a, h * HALF : (h + 1) * HALF], in_=done[:])
 
         gather_scales(5, "got_scale")
-        for c in (0, LAST):
+        for c in (0, 2, LAST):
             interleave(scalar_copy, c)
         quantize(0)
-        for c in range(1, LAST):
-            interleave(nc.vector.tensor_copy, c)
+        interleave(nc.vector.tensor_copy, 1)
         for c in range(1, CHUNKS):
             quantize(c)
-        gather_scales(3, "x_bf1")
+        gather_scales(3, "x_rest")
 
         skip_nj = keep.tile([P, TILES, LAST * P], F32, name="skip_nj")
         for c in range(LAST):

@@ -82,9 +82,9 @@ def tile_list_interp_res_kernel(tc, tab_words, tab_scales, w_words, w_scales, x,
 
         nc.sync.dma_start(out=x_lead[:], in_=x_view[:, :, 0:P])
         nc.sync.dma_start(offsets[:], offs)
+        nc.sync.dma_start(out=wx_codes[:], in_=wx_words[0].bitcast(I32))
         load_scales(tab_scale, tab_scales)
         nc.sync.dma_start(out=x_rest[:], in_=x_view[:, :, P:J])
-        nc.sync.dma_start(out=wx_codes[:], in_=wx_words[0].bitcast(I32))
         load_scales(wx_scale, wx_scales)
         nc.sync.dma_start(out=tab_codes[:], in_=tab_words[0].rearrange("p t i -> p (t i)").bitcast(I32))
         nc.sync.dma_start(out=iw_rows[0:CHUNKS, :], in_=iw0.rearrange("(c p) -> c p", p=P))
@@ -116,10 +116,10 @@ def tile_list_interp_res_kernel(tc, tab_words, tab_scales, w_words, w_scales, x,
         def gather_codes(g, h):
             nc.vector.tensor_copy(got_codes[g][h][:], tab_codes[:].bitcast(U32).indirect(list_slice(g, h)))
 
-        def interleave(copy, c):
+        def interleave(copy, c, cols=slice(0, P)):
             copy(
-                out=x_bf[c].rearrange("p (s i) t -> p s t i", i=4),
-                in_=x_raw[c].rearrange("p t (s i) -> p s t i", i=4),
+                out=x_bf[c][:, cols, :].rearrange("p (s i) t -> p s t i", i=4),
+                in_=x_raw[c][:, :, cols].rearrange("p t (s i) -> p s t i", i=4),
             )
 
         def quantize(c):
@@ -179,14 +179,16 @@ def tile_list_interp_res_kernel(tc, tab_words, tab_scales, w_words, w_scales, x,
             nc.vector.tensor_tensor(done[:], sums[SUM_BANKS[h][a]][:, a % 2, :], addend, ADD)
             nc.sync.dma_start(out=out_view[:, a, h * HALF : (h + 1) * HALF], in_=done[:])
 
-        gather_scales(5, "got_scale")
-        for c in (0, 2, LAST):
-            interleave(scalar_copy, c)
+        gather_scales(6, "got_scale")
+        interleave(scalar_copy, 0)
         quantize(0)
+        interleave(scalar_copy, 2, slice(P // 2, P))
+        interleave(scalar_copy, LAST)
         interleave(nc.vector.tensor_copy, 1)
+        interleave(nc.vector.tensor_copy, 2, slice(0, P // 2))
         for c in range(1, CHUNKS):
             quantize(c)
-        gather_scales(3, "x_rest")
+        gather_scales(2, "x_rest")
 
         skip_nj = keep.tile([P, TILES, LAST * P], F32, name="skip_nj")
         for c in range(LAST):

from contextlib import ExitStack

import concourse.mybir as mybir
from concourse.masks import make_identity

K, L, N, T, J = 512, 512, 512, 2048, 512
FLOPS = 2 * (2 * K + L) * N * J

F32 = mybir.dt.float32
BF16 = mybir.dt.bfloat16
I32 = mybir.dt.int32
U32 = mybir.dt.uint32
U16 = mybir.dt.uint16
U8 = mybir.dt.uint8
FP8X4 = mybir.dt.float8_e4m3fn_x4
FP4X4 = mybir.dt.float4_e2m1fn_x4
COPY = mybir.ActivationFunctionType.Copy
MULT = mybir.AluOpType.mult
ADD = mybir.AluOpType.add

P = 128
PACK = 4
GROUP = 16
QUADRANT = 32
HALF = J // 2
CHUNKS = J // P
LAST = CHUNKS - 1
TILES = N // P
PAIRS = (range(0, 2), range(2, 4))
PAIR_COLS = (slice(0, N // 2), slice(N // 2, N))

SKIP_BANKS = (2, 3, 4, 5)
WEIGHT_BANK = SKIP_BANKS[0]
PRODUCT_BANKS = ((6, 7, 2, 3), (0, 1, 4, 5))
SUM_BANKS = ((6, 6, 7, 7), (0, 0, 1, 2))


def tile_list_interp_res_kernel(tc, tab_words, tab_scales, w_words, w_scales, x, wx_words, wx_scales, iw0, iw1, res, offs, out):
    nc = tc.nc
    with ExitStack() as ctx:
        keep = ctx.enter_context(tc.tile_pool(name="keep", bufs=1))
        banks = ctx.enter_context(tc.psum_pool(name="banks", bufs=1))

        offsets = keep.tile([P, 2 * J // GROUP], U16, name="offsets")
        tab_scale = keep.tile([P, T // 4], I32, name="tab_scale", align_bytes=64)
        w_scale = keep.tile([P, N // 4], I32, name="w_scale", align_bytes=64)
        wx_scale = keep.tile([P, N // 4], I32, name="wx_scale", align_bytes=64)
        tab_codes = keep.tile([P, T], I32, name="tab_codes", align_bytes=64)
        w_codes = keep.tile([P, N], I32, name="w_codes", align_bytes=64)
        wx_codes = keep.tile([P, N // 2], I32, name="wx_codes", align_bytes=64)
        ident = keep.tile([P, P], F32, name="ident")
        iw_rows = keep.tile([P, P], F32, name="iw_rows")
        iw_cols = [keep.tile([P, CHUNKS], F32, name=f"iw_cols{g}") for g in range(2)]
        x_lead = keep.tile([P, PACK, P], F32, name="x_lead")
        x_rest = keep.tile([P, PACK, J - P], F32, name="x_rest", align_bytes=64)
        x_raw = [x_lead[:]] + [x_rest[:, :, c * P : (c + 1) * P] for c in range(CHUNKS - 1)]
        x_bf = [keep.tile([P, P, PACK], BF16, name=f"x_bf{c}", align_bytes=64)[:] for c in range(CHUNKS)]
        x_codes = [keep.tile([P, HALF], U32, name=f"x_codes{h}", align_bytes=64) for h in range(2)]
        x_scale = [keep.tile([P, HALF], U8, name=f"x_scale{h}", align_bytes=64) for h in range(2)]
        res_parts = ((0, slice(0, 2)), (0, slice(2, TILES)), (1, slice(0, TILES)))
        res_sb = [keep.tile([P, rows.stop - rows.start, HALF], F32, name=f"res_sb{h}{rows.start}") for h, rows in res_parts]
        got_codes = [[keep.tile([P, HALF], U32, name=f"got_codes{g}{h}", align_bytes=64) for h in range(2)] for g in range(2)]
        got_scale = []
        sums = {}

        def load_scales(tile, scales):
            rows = scales[0].bitcast(I32)
            for r in range(4):
                nc.sync.dma_start(out=tile[r:P:QUADRANT, :], in_=rows[r:16:4, :])

        x_view = x.rearrange("(p t) j -> p t j", t=PACK)
        res_view = res.rearrange("(a p) j -> p a j", p=P)
        out_view = out.rearrange("(a p) j -> p a j", p=P)

        nc.vector.memset(tab_scale[:, 0 : T // 8], 0)
        nc.gpsimd.memset(tab_scale[:, T // 8 : T // 4], 0)
        nc.vector.memset(wx_scale[:], 0)
        nc.vector.memset(w_scale[:], 0)
        nc.vector.memset(iw_rows[:], 0.0)
        nc.vector.memset(ident[:], 0.0)
        make_identity(nc, ident[:], nomemset=True)

        nc.sync.dma_start(out=x_lead[:], in_=x_view[:, :, 0:P])
        nc.sync.dma_start(offsets[:], offs)
        nc.sync.dma_start(out=wx_codes[:], in_=wx_words[0].bitcast(I32))
        load_scales(tab_scale, tab_scales)
        nc.sync.dma_start(out=x_rest[:], in_=x_view[:, :, P:J])
        load_scales(wx_scale, wx_scales)
        nc.sync.dma_start(out=tab_codes[:], in_=tab_words[0].rearrange("p t i -> p (t i)").bitcast(I32))
        nc.sync.dma_start(out=iw_rows[0:CHUNKS, :], in_=iw0.rearrange("(c p) -> c p", p=P))
        nc.sync.dma_start(out=w_codes[:], in_=w_words[0].rearrange("p n i -> p (n i)").bitcast(I32))
        load_scales(w_scale, w_scales)
        for i, (h, rows) in enumerate(res_parts):
            nc.sync.dma_start(out=res_sb[i][:], in_=res_view[:, rows, h * HALF : (h + 1) * HALF])
            if i == 0:
                with nc.allow_non_contiguous_dma(reason="one weight a partition and chunk"):
                    nc.sync.dma_start(out=iw_cols[1][:], in_=iw1.rearrange("(c p) -> p c", p=P))

        def scalar_copy(out, in_):
            nc.scalar.activation(out=out, in_=in_, func=COPY)

        def in_half(c):
            return slice((c % 2) * P, (c % 2 + 1) * P)

        def list_slice(g, h):
            column = (g * J + h * HALF) // GROUP
            return offsets[:, column : column + HALF // GROUP]

        def gather_scales(count, tag):
            first = len(got_scale)
            got = keep.tile([P, count * P], U8, name=tag, align_bytes=64)
            entries = offsets[:, first * P // GROUP : (first + count) * P // GROUP]
            nc.vector.tensor_copy(got[:], tab_scale[:].bitcast(U8).indirect(entries))
            got_scale.extend(got[:, i * P : (i + 1) * P] for i in range(count))

        def gather_codes(g, h):
            nc.vector.tensor_copy(got_codes[g][h][:], tab_codes[:].bitcast(U32).indirect(list_slice(g, h)))

        def interleave(copy, c, cols=slice(0, P)):
            copy(
                out=x_bf[c][:, cols, :].rearrange("p (s i) t -> p s t i", i=4),
                in_=x_raw[c][:, :, cols].rearrange("p t (s i) -> p s t i", i=4),
            )

        def quantize(c):
            nc.vector.quantize_mx(
                out=x_codes[c // 2][:, in_half(c)].bitcast(FP8X4),
                scales=x_scale[c // 2][:, in_half(c)],
                in_=x_bf[c].rearrange("p j t -> p (j t)"),
            )

        def product_jn(codes, scale, moving, moving_scale, bank):
            acc = banks.tile([P, N], F32, name=f"bank{bank}")
            nc.tensor.matmul_mx(
                out=acc[:],
                lhsT=codes.bitcast(FP8X4),
                lhsT_scale=scale,
                rhs=moving,
                rhs_scale=moving_scale[:].bitcast(U8),
                start=True,
                stop=True,
            )
            return acc

        def skip_product_nj(c):
            acc = banks.tile([P, TILES, P], F32, name=f"bank{SKIP_BANKS[c]}")
            for a in range(TILES):
                nc.tensor.matmul_mx(
                    out=acc[:, a, :],
                    lhsT=wx_codes[:, a * P // 2 : (a + 1) * P // 2].bitcast(FP4X4),
                    lhsT_scale=wx_scale[:].bitcast(U8)[:, a * P : (a + 1) * P],
                    rhs=x_codes[c // 2][:, in_half(c)].bitcast(FP8X4),
                    rhs_scale=x_scale[c // 2][:, in_half(c)],
                    start=True,
                    stop=True,
                )
            return acc

        def turn(term, c, tiles, opens=(), closes=()):
            for a in tiles:
                bank = SUM_BANKS[c // 2][a]
                if a in opens:
                    sums[bank] = banks.tile([P, 2, HALF], F32, name=f"bank{bank}")
                nc.tensor.matmul(
                    out=sums[bank][:, a % 2, in_half(c)],
                    lhsT=term[:, a * P : (a + 1) * P],
                    rhs=ident[:],
                    is_transpose=True,
                    start=a in opens,
                    stop=a in closes,
                )

        def weight(g, c):
            return iw_cols[g][:, c : c + 1]

        def finish(h, a):
            done = keep.tile([P, HALF], F32, name=f"done{h}{a}")
            addend = res_sb[a // 2][:, a % 2, :] if h == 0 else res_sb[2][:, a, :]
            nc.vector.tensor_tensor(done[:], sums[SUM_BANKS[h][a]][:, a % 2, :], addend, ADD)
            nc.sync.dma_start(out=out_view[:, a, h * HALF : (h + 1) * HALF], in_=done[:])

        gather_scales(6, "got_scale")
        interleave(scalar_copy, 0)
        quantize(0)
        interleave(scalar_copy, 2, slice(P // 2, P))
        interleave(scalar_copy, LAST)
        interleave(nc.vector.tensor_copy, 1)
        interleave(nc.vector.tensor_copy, 2, slice(0, P // 2))
        for c in range(1, CHUNKS):
            quantize(c)
        gather_scales(2, "x_rest")

        skip_nj = keep.tile([P, TILES, LAST * P], F32, name="skip_nj")
        for c in range(LAST):
            acc = skip_product_nj(c)
            scalar_copy(out=skip_nj[:, :, c * P : (c + 1) * P], in_=acc[:])
        acc = product_jn(x_codes[1][:, in_half(LAST)], x_scale[1][:, in_half(LAST)], wx_codes[:].bitcast(FP4X4), wx_scale, SKIP_BANKS[LAST])
        skip_jn = keep.tile([P, N], F32, name=f"skip{LAST}")
        scalar_copy(out=skip_jn[:], in_=acc[:])

        iw_acc = banks.tile([P, N], F32, name=f"bank{WEIGHT_BANK}")
        nc.tensor.transpose(iw_acc[:, 0:P], iw_rows[:], ident[:])
        scalar_copy(out=iw_cols[0][:], in_=iw_acc[:, 0:CHUNKS])

        for h in range(2):
            for g in range(2):
                gather_codes(g, h)

        for pair in range(2):
            nc.gpsimd.tensor_tensor(res_sb[pair][:], skip_nj[:, 2 * pair : 2 * pair + 2, 0:HALF], res_sb[pair][:], ADD)
        nc.gpsimd.tensor_tensor(res_sb[2][:, :, 0:P], skip_nj[:, :, HALF : HALF + P], res_sb[2][:, :, 0:P], ADD)

        products = {}
        for h in range(2):
            for g in range(2):
                for c in (2 * h, 2 * h + 1):
                    products[g, c] = product_jn(got_codes[g][h][:, in_half(c)], got_scale[CHUNKS * g + c], w_codes[:].bitcast(FP8X4), w_scale, PRODUCT_BANKS[g][c])

        def scaled(term, g, c, cols):
            nc.scalar.activation(out=term[:, cols], in_=products[g, c][:, cols], func=COPY, scale=weight(g, c))

        def fused(term, g, c, cols, other):
            nc.vector.scalar_tensor_tensor(term[:, cols], products[g, c][:, cols], weight(g, c), other[:, cols], MULT, ADD)

        terms = {}
        for c in range(LAST):
            terms[0, c] = keep.tile([P, N], F32, name=f"term0{c}")
            scaled(terms[0, c], 0, c, slice(0, N))
        upper = keep.tile([P, N], F32, name="upper")
        scaled(upper, 0, LAST, slice(P, N))
        for c in (LAST, 2):
            terms[1, c] = keep.tile([P, N], F32, name=f"term1{c}")
        for cols in PAIR_COLS:
            for c in (LAST, 2):
                scaled(terms[1, c], 1, c, cols)

        both = [keep.tile([P, N], F32, name=f"term1{c}") for c in range(2)]
        for cols in PAIR_COLS:
            for c in range(2):
                fused(both[c], 1, c, cols, terms[0, c])
        lower = keep.tile([P, N], F32, name="term00")
        fused(lower, 0, LAST, slice(0, P), skip_jn)

        for tiles in PAIRS:
            turn(both[0], 0, tiles, opens=(tiles[0],))
            turn(both[1], 1, tiles, closes=(tiles[-1],))
        for a in range(TILES):
            finish(0, a)

        first, second = PAIRS
        turn(terms[0, 2], 2, first, opens=(first[0],))
        turn(skip_jn, LAST, first[1:])
        turn(upper, LAST, first[1:])
        turn(lower, LAST, first[:1])
        turn(terms[1, LAST], LAST, first)
        turn(terms[1, 2], 2, first, closes=(first[-1],))
        turn(skip_jn, LAST, second, opens=second)
        turn(upper, LAST, second)
        turn(terms[0, 2], 2, second)
        turn(terms[1, LAST], LAST, second)
        turn(terms[1, 2], 2, second, closes=second)
        for a in range(TILES):
            finish(1, a)
